import numpy as np
import ml_dtypes


def mxq(x, axis, fmt="e4m3"):
    dtype, down = {"e4m3": (ml_dtypes.float8_e4m3fn, 7), "e5m2": (ml_dtypes.float8_e5m2, 14)}[fmt]
    v = np.moveaxis(np.asarray(x, np.float32).astype(ml_dtypes.bfloat16).astype(np.float64), axis, -1)
    blocks = v.reshape(v.shape[:-1] + (-1, 32))
    amax = np.abs(blocks).max(-1, keepdims=True)
    byte = np.maximum(np.where(amax > 0, np.frexp(amax)[1] - 1 + 127, 0) - down, 1)
    scale = np.exp2(byte - 127.0)
    codes = (blocks / scale).astype(np.float32).astype(dtype).astype(np.float64)
    return np.moveaxis((codes * scale).reshape(v.shape), -1, axis)


WIDE = False


def mx_kscale(k):
    if not WIDE:
        return np.ones(k)
    levels = np.array([10, -10, 5, -5, 0])
    if k % 512:
        return np.exp2(np.random.permutation(np.resize(levels, k // 32))).repeat(32)
    a = np.empty((k // 512, 16))
    for p in range(k // 512):
        a[p, :8] = np.random.permutation(np.resize(levels, 8))
        for g in range(8):
            far = levels[np.abs(levels - a[p, g]) >= 10]
            a[p, g + 8] = far[np.random.randint(len(far))]
    return np.exp2(a.ravel()).repeat(32)


BF16 = ml_dtypes.bfloat16


def bf(x):
    return np.asarray(x, np.float32).astype(BF16)


def f64(x):
    return np.asarray(x).astype(np.float64)


E2M1 = np.array([0.0, 0.5, 1.0, 1.5, 2.0, 3.0, 4.0, 6.0, -0.0, -0.5, -1.0, -1.5, -2.0, -3.0, -4.0, -6.0])


def pack_weight(w, fmt):
    k, n = w.shape
    w = f64(bf(w)).reshape(k // 32, 32, n)
    amax = np.abs(w).max(1)
    if fmt == "e4m3":
        byte = np.frexp(amax)[1] - 1 + 127 - 7
    else:
        mant, ex = np.frexp(amax / 6.0)
        byte = np.where(mant > 0.5, ex, ex - 1) + 127
    byte = np.clip(np.where(amax > 0, byte, 1), 1, 254)
    scaled = (w * np.exp2(127.0 - byte)[:, None, :]).reshape(k, n).astype(np.float32)
    by_word = np.ascontiguousarray(scaled.reshape(k // 512, 128, 4, n).transpose(0, 1, 3, 2))
    if fmt == "e4m3":
        words = by_word.astype(ml_dtypes.float8_e4m3fn).view(np.uint8)
    else:
        c = by_word.astype(ml_dtypes.float4_e2m1fn).view(np.uint8) & 0xF
        words = c[..., 0::2] | (c[..., 1::2] << 4)
    return np.ascontiguousarray(words), np.ascontiguousarray(byte.astype(np.uint8).reshape(k // 512, 16, n))


def unpack_weight(words, scales, fmt):
    g, p, n, _ = words.shape
    if fmt == "e4m3":
        vals = np.ascontiguousarray(words).view(ml_dtypes.float8_e4m3fn).astype(np.float64)
    else:
        nib = np.empty((g, p, n, 4), np.uint8)
        nib[..., 0::2] = words & 0xF
        nib[..., 1::2] = words >> 4
        vals = E2M1[nib]
    vals = vals * np.repeat(np.exp2(scales.astype(np.float64) - 127.0), 8, axis=1)[..., None]
    return vals.transpose(0, 1, 3, 2).reshape(g * 512, n)
def pack4(w):
    words, scales = pack_weight(w, "e2m1")
    return words.reshape(words.shape[0], 128, -1), scales


def unpack4(words, scales):
    return unpack_weight(words.reshape(words.shape[0], 128, -1, 2), scales, "e2m1")


def planes(Y):
    n, m = Y.shape
    b = f64(bf(Y)).reshape(n // 32, 32, m)
    amax = np.abs(b).max(1)
    byte = np.clip(np.where(amax > 0, np.frexp(amax)[1] - 1 + 127 - 7, 1), 1, 254)
    codes = (b * np.exp2(127.0 - byte)[:, None, :]).reshape(n, m).astype(np.float32).astype(ml_dtypes.float8_e4m3fn).view(np.uint8)
    words = codes.reshape(n // 512, 128, 4, m).transpose(0, 1, 3, 2)
    return np.ascontiguousarray(words), np.ascontiguousarray(byte.astype(np.uint8).reshape(n // 512, 16, m))


P, T, D, H, Q, R = 1280, 2048, 1024, 512, 1536, 8

def sinusoids(dates):
    phase = 2.0 * np.pi * dates[:, None] * np.arange(1, H // 2 + 1) / R
    return np.sqrt(2.0 / T) * np.concatenate([np.cos(phase), np.sin(phase)], axis=1)

def setup_inputs():
    s, d, t = mx_kscale(T), mx_kscale(D), mx_kscale(H)
    fit_dates = R * (np.arange(T) + np.random.rand(T)) / T
    held_dates = R * (np.arange(Q) + np.random.rand(Q)) / Q
    prior_words, prior_scales = pack4(np.random.randn(D, H) / np.sqrt(D) / d[:, None])
    return {
        "series": bf(1.5 * np.random.randn(P, T) * s),
        "waves_fit": bf(sinusoids(fit_dates) / s[:, None]),
        "site": bf(np.random.randn(P, D) * d),
        "prior_words": prior_words,
        "prior_scales": prior_scales,
        "shrink": bf(t / (1.0 + 0.3 * np.exp(0.5 * np.random.randn(H)))),
        "waves_held": bf(sinusoids(held_dates).T / t[:, None]),
        "held": bf(0.8 * np.random.randn(P, Q)),
        "inv_spread": bf(0.8 * np.exp(0.2 * np.random.randn(P))),
        "date_weight": bf(np.exp(0.8 * np.random.randn(Q))),
    }

def reference(series, waves_fit, site, prior_words, prior_scales, shrink, waves_held, held, inv_spread, date_weight):
    seen = mxq(f64(series), 1, "e4m3") @ mxq(f64(waves_fit), 0, "e4m3")
    expected = mxq(f64(site), 1, "e4m3") @ unpack4(prior_words, prior_scales)
    coef = (seen + expected) * f64(shrink)
    curve = mxq(coef, 1, "e4m3") @ mxq(f64(waves_held), 0, "e4m3")
    y = np.tanh((f64(held) - curve) * f64(inv_spread)[:, None]) * f64(date_weight)
    Y = y.T
    words, scales = planes(Y)
    return y, words, scales

@@ -1,0 +1,700 @@
+from contextlib import ExitStack
+
+import concourse.mybir as mybir
+from concourse.masks import make_identity
+
+NPIX, T, D, H, Q = 1280, 2048, 1024, 512, 1536
+FLOPS = 2 * NPIX * (T * H + D * H + H * Q)
+
+F32 = mybir.dt.float32
+BF16 = mybir.dt.bfloat16
+I32 = mybir.dt.int32
+U32 = mybir.dt.uint32
+U8 = mybir.dt.uint8
+FP8X4 = mybir.dt.float8_e4m3fn_x4
+FP4X4 = mybir.dt.float4_e2m1fn_x4
+ALU = mybir.AluOpType
+ACT = mybir.ActivationFunctionType
+
+P = 128
+KP = 512
+TILES = NPIX // P
+GT, GD, GQ = T // KP, D // KP, Q // KP
+
+
+def tile_harmonic_phenology_anomaly_k6_kernel(
+    tc, series, waves_fit, site, prior_words, prior_scales, shrink, waves_held, held,
+    inv_spread, date_weight, out_0, out_1, out_2,
+):
+    nc = tc.nc
+    with ExitStack() as ctx:
+        keep = ctx.enter_context(tc.tile_pool(name="keep", bufs=1))
+        work = ctx.enter_context(tc.tile_pool(name="work", bufs=2))
+        psum = ctx.enter_context(tc.psum_pool(name="psum", bufs=1))
+        ctx.enter_context(tc.manual_schedule())
+
+        def bank(k, dtype=F32):
+            width = 512 if dtype == F32 else 1024
+            return psum.tile([P, width], dtype, name="bank%d" % k, tag="bank%d" % k)
+
+        ident = keep.tile([P, P], F32, name="ident")
+        ident_bf = keep.tile([P, P], BF16, name="ident_bf")
+        const_rows = keep.tile([P, P], BF16, name="const_rows")
+        const_cols = keep.tile([P, 16], F32, name="const_cols")
+        weight_cols = keep.tile([P, 16], BF16, name="weight_cols")
+        warm = keep.tile([P, 8], F32, name="warm")
+        weight_bc = keep.tile([P, Q], BF16, name="weight_bc")
+        pw_raw = keep.tile([P, GD, 2 * H], U8, name="pw_raw", align_bytes=64)
+        ps_raw = keep.tile([P, GD, H], U8, name="ps_raw", align_bytes=64)
+        pw = keep.tile([P, GD, 2 * H], U8, name="pw", align_bytes=64)
+        ps = keep.tile([P, GD, H], U8, name="ps", align_bytes=64)
+        wf_raw = keep.tile([P, GT, 4, H], BF16, name="wf_raw", align_bytes=64)
+        wf_codes = keep.tile([P, GT, H], U32, name="wf_codes", align_bytes=64)
+        wf_scales = keep.tile([P, GT, H], U8, name="wf_scales", align_bytes=64)
+        wh_raw = keep.tile([P, 4, Q], BF16, name="wh_raw", align_bytes=64)
+        wh_codes = keep.tile([P, Q], U32, name="wh_codes", align_bytes=64)
+        wh_scales = keep.tile([P, Q], U8, name="wh_scales", align_bytes=64)
+        y_codes = keep.tile([P, GQ, NPIX], U32, name="y_codes", align_bytes=64)
+        y_scales = keep.tile([P, GQ, NPIX], U8, name="y_scales", align_bytes=64)
+        w_grouped = keep.tile([P, GT + GQ, 4 * KP], BF16, name="w_grouped", align_bytes=64)
+
+        t = {}
+
+        def px(i):
+            return slice(i * P, (i + 1) * P)
+
+        def grp(g):
+            return slice(g * KP, (g + 1) * KP)
+
+        def load_series(i):
+            t["series", i] = work.tile([P, T], BF16, name="series_t", bufs=4)
+            nc.sync.dma_start(out=t["series", i][:], in_=series[px(i), :])
+
+        def load_site(i):
+            t["site", i] = work.tile([P, D], BF16, name="site_t", bufs=4)
+            nc.sync.dma_start(out=t["site", i][:], in_=site[px(i), :])
+
+        def load_held(i):
+            t["held", i] = work.tile([P, Q], BF16, name="held_t", bufs=4)
+            nc.sync.dma_start(out=t["held", i][:], in_=held[px(i), :])
+
+        def load_wf(g):
+            nc.sync.dma_start(out=wf_raw[:, g, :, :], in_=waves_fit[grp(g), :].rearrange("(p j) h -> p j h", j=4))
+
+        def load_prior_words():
+            nc.sync.dma_start(out=pw_raw[:].bitcast(I32), in_=prior_words.rearrange("g p b -> p g b").bitcast(I32))
+
+        def load_wh(g0, g1):
+            cols = slice(g0 * KP, g1 * KP)
+            rows = waves_held.rearrange("(a t r) q -> r a t q", t=4, r=4)
+            for r in range(4):
+                nc.sync.dma_start(out=wh_raw[r:P:4, :, cols], in_=rows[r, :, :, cols])
+
+        def copy_on(engine, out, in_):
+            if engine == "vector":
+                nc.vector.tensor_copy(out=out, in_=in_)
+            elif engine == "gpsimd":
+                nc.gpsimd.tensor_scalar(out=out, in0=in_, scalar1=1.0, scalar2=-0.0, op0=ALU.mult, op1=ALU.add)
+            else:
+                nc.scalar.copy(out=out, in_=in_)
+
+        def group_wf(g, half, engine):
+            ts = slice(2 * half, 2 * half + 2)
+            dst = w_grouped[:, g, :].rearrange("p (t a r j) -> p t a j r", t=4, r=4, j=4)
+            src = wf_raw[:, g, :, :].rearrange("p j (a t r) -> p t a j r", t=4, r=4)
+            copy_on(engine, dst[:, ts], src[:, ts])
+
+        def quant_wf(g):
+            nc.vector.quantize_mx(out=wf_codes[:, g, :].bitcast(FP8X4), scales=wf_scales[:, g, :], in_=w_grouped[:, g, :])
+
+        def group_wh(g, half, engine):
+            cs = slice(64 * half, 64 * half + 64)
+            dst = w_grouped[:, GT + g, :].rearrange("p (c i t) -> p c t i", i=4, t=4)
+            src = wh_raw[:, :, grp(g)].rearrange("p t (c i) -> p c t i", i=4)
+            copy_on(engine, dst[:, cs], src[:, cs])
+
+        def quant_wh(g):
+            nc.vector.quantize_mx(out=wh_codes[:, grp(g)].bitcast(FP8X4), scales=wh_scales[:, grp(g)], in_=w_grouped[:, GT + g, :])
+
+        def order_prior():
+            for g in range(GD):
+                nc.vector.tensor_copy(
+                    out=pw[:, g, :].bitcast(I32).rearrange("p (t a w) -> p t a w", t=4, w=2),
+                    in_=pw_raw[:, g, :].bitcast(I32).rearrange("p (a t w) -> p t a w", t=4, w=2))
+            nc.vector.tensor_copy(
+                out=ps[:].bitcast(I32).rearrange("p g (t a) -> p g t a", t=4),
+                in_=ps_raw[:].bitcast(I32).rearrange("p g (a t) -> p g t a", t=4))
+
+        def turn_x(i, b, k):
+            src = t["series", i] if b < 2 else t["site", i]
+            words = src[:].bitcast(F32)
+            g0 = 2 * b if b < 2 else 0
+            pt = bank(k)
+            t["xt", i, b] = pt
+            for gg in range(2):
+                for u in range(2):
+                    lo = 256 * (g0 + gg)
+                    col = (2 * gg + u) * P
+                    nc.tensor.transpose(pt[:, col:col + P], words[:, lo + u:lo + 256:2], ident[:])
+
+        def copy_x(i, b, engine):
+            if b == 0:
+                t["xg", i] = work.tile([P, T + D], BF16, name="xg", align_bytes=64)
+            xg_words = t["xg", i][:].bitcast(F32)
+            copy_on(engine,
+                    xg_words[:, 512 * b:512 * (b + 1)].rearrange("p (g m u) -> p g m u", g=2, u=2),
+                    t["xt", i, b][:].rearrange("p (g u m) -> p g m u", g=2, u=2))
+
+        def x_tiles(i):
+            if ("xc", i) not in t:
+                t["xc", i] = work.tile([P, (GT + GD) * P], U32, name="xc", align_bytes=64, bufs=3)
+                t["xs", i] = work.tile([P, (GT + GD) * P], U8, name="xs", align_bytes=64, bufs=3)
+
+        def quant_series(i):
+            x_tiles(i)
+            nc.vector.quantize_mx(out=t["xc", i][:, 0:GT * P].bitcast(FP8X4), scales=t["xs", i][:, 0:GT * P], in_=t["xg", i][:, 0:T])
+
+        def quant_site(i):
+            x_tiles(i)
+            nc.vector.quantize_mx(out=t["xc", i][:, GT * P:].bitcast(FP8X4), scales=t["xs", i][:, GT * P:], in_=t["xg", i][:, T:])
+
+        def stage1(i, k):
+            acc = bank(k)
+            t["acc", i] = acc
+            xc, xs = t["xc", i], t["xs", i]
+            for s in range(4):
+                for g in range(GT + GD):
+                    if g < GT:
+                        lhsT, lhsT_scale = wf_codes[:, g, px(s)].bitcast(FP8X4), wf_scales[:, g, px(s)]
+                    else:
+                        lhsT = pw[:, g - GT, 2 * P * s:2 * P * (s + 1)].bitcast(FP4X4)
+                        lhsT_scale = ps[:, g - GT, px(s)]
+                    nc.tensor.matmul_mx(out=acc[:, px(s)], lhsT=lhsT, lhsT_scale=lhsT_scale,
+                                        rhs=xc[:, px(g)].bitcast(FP8X4), rhs_scale=xs[:, px(g)],
+                                        start=(g == 0), stop=(g == GT + GD - 1))
+
+        def shrink_coef(i):
+            t["coef", i] = work.tile([P, H], BF16, name="coef", align_bytes=64)
+            nc.vector.tensor_tensor(
+                out=t["coef", i][:].rearrange("p (m s) -> p m s", s=4),
+                in0=t["acc", i][:].rearrange("p (s m) -> p m s", s=4),
+                in1=const_cols[:, 0:4].unsqueeze(1).to_broadcast([P, P, 4]),
+                op=ALU.mult)
+
+        def quant_coef(i):
+            t["cc", i] = work.tile([P, P], U32, name="cc", align_bytes=64, bufs=3)
+            t["cs", i] = work.tile([P, P], U8, name="cs", align_bytes=64, bufs=3)
+            nc.vector.quantize_mx(out=t["cc", i][:].bitcast(FP8X4), scales=t["cs", i][:], in_=t["coef", i][:])
+
+        def curve(i, g, k):
+            t["curve", i, g] = bank(k)
+            nc.tensor.matmul_mx(out=t["curve", i, g][:], lhsT=t["cc", i][:].bitcast(FP8X4), lhsT_scale=t["cs", i][:],
+                                rhs=wh_codes[:, grp(g)].bitcast(FP8X4), rhs_scale=wh_scales[:, grp(g)],
+                                start=True, stop=True)
+
+        def subtract(i, g):
+            if g == 0:
+                t["diff", i] = work.tile([P, Q], F32, name="diff")
+            nc.vector.tensor_tensor(out=t["diff", i][:, grp(g)], in0=t["held", i][:, grp(g)], in1=t["curve", i, g][:], op=ALU.subtract)
+
+        def bound(i, g):
+            if g == 0:
+                t["tanh", i] = work.tile([P, Q], F32, name="tanh")
+            nc.scalar.activation(out=t["tanh", i][:, grp(g)], in_=t["diff", i][:, grp(g)], func=ACT.Tanh,
+                                 scale=const_cols[:, 4 + i:5 + i])
+
+        def weigh(i, g, engine=nc.vector):
+            if g == 0:
+                t["y", i] = work.tile([P, Q], F32, name="y", bufs=3)
+            engine.tensor_tensor(out=t["y", i][:, grp(g)], in0=t["tanh", i][:, grp(g)], in1=weight_bc[:, grp(g)], op=ALU.mult)
+
+        def store_y(i, g0, g1):
+            cols = slice(g0 * KP, g1 * KP)
+            nc.sync.dma_start(out=out_0[px(i), cols], in_=t["y", i][:, cols])
+
+        def round_y(i, g, engine):
+            if g == 0:
+                t["yb", i] = work.tile([P, Q], BF16, name="yb")
+            copy_on(engine,
+                    t["yb", i][:, grp(g)].rearrange("m (u p e) -> m u p e", u=2, e=2),
+                    t["y", i][:, grp(g)].rearrange("m (p u e) -> m u p e", u=2, e=2))
+
+        def turn_y(i, g0, g1, k):
+            words = t["yb", i][:].bitcast(F32)
+            pt = bank(k)
+            t["ytp", i, g0] = pt
+            for j in range(2 * g0, 2 * g1):
+                nc.tensor.transpose(pt[:, px(j - 2 * g0)], words[:, px(j)], ident[:])
+
+        def copy_y(i, g0, g1, engine):
+            if g0 == 0:
+                t["yt", i] = work.tile([P, Q], BF16, name="yt", align_bytes=64)
+            yt_words = t["yt", i][:].bitcast(F32)
+            copy_on(engine,
+                    yt_words[:, 2 * g0 * P:2 * g1 * P].rearrange("p (g m u) -> p g m u", m=P, u=2),
+                    t["ytp", i, g0][:, 0:2 * (g1 - g0) * P].rearrange("p (g u m) -> p g m u", m=P, u=2))
+
+        def quant_y(i, g):
+            nc.vector.quantize_mx(out=y_codes[:, g, px(i)].bitcast(FP8X4), scales=y_scales[:, g, px(i)], in_=t["yt", i][:, grp(g)])
+
+        def turn_consts(k):
+            t["consts"] = bank(k, BF16)
+            nc.tensor.transpose(t["consts"][:, 0:P], const_rows[:], ident_bf[:])
+
+        def copy_consts():
+            nc.scalar.copy(out=weight_cols[:], in_=t["consts"][:, 16:32])
+            nc.scalar.copy(out=const_cols[:], in_=t["consts"][:, 0:16])
+
+        def spread_weight(g, k):
+            t["wt", g] = bank(k, BF16)
+            for c in range(4):
+                nc.tensor.transpose(t["wt", g][:, px(c)], weight_cols[:, 4 * g + c:4 * g + c + 1].to_broadcast([P, P]), ident_bf[:])
+
+        def copy_weight(g, engine):
+            copy_on(engine, weight_bc[:, grp(g)], t["wt", g][:, 0:KP])
+
+        def store_codes(i0, i1):
+            cols = slice(i0 * P, i1 * P)
+            dst = out_1.rearrange("g p m t -> p g (m t)")[:, :, 4 * i0 * P:4 * i1 * P].bitcast(I32)
+            nc.sync.dma_start(out=dst, in_=y_codes[:, :, cols].bitcast(I32))
+
+        def store_scales(i0, i1):
+            cols = slice(i0 * P, i1 * P)
+            for q in range(4):
+                nc.sync.dma_start(out=out_2[:, 4 * q:4 * q + 4, cols].rearrange("g r m -> r g m").bitcast(I32),
+                                  in_=y_scales[32 * q:32 * q + 4, :, cols].bitcast(I32))
+
+        def load_prior_scales(engine, q):
+            engine.dma_start(out=ps_raw[32 * q:32 * q + 4, :, :].bitcast(I32),
+                             in_=prior_scales[:, 4 * q:4 * q + 4, :].rearrange("g r n -> r g n").bitcast(I32))
+
+        nc.vector.memset(const_rows[:], 0.0)
+        nc.vector.memset(ps_raw[:].bitcast(I32), 0)
+        nc.vector.memset(warm[:], 0.0)
+        make_identity(nc, ident[:])
+        nc.vector.tensor_copy(out=ident_bf[:], in_=ident[:])
+        load_wf(0)
+        nc.scalar.dma_start(out=const_rows[0:4, :].rearrange("t (a r) -> t a r", r=4),
+                            in_=shrink.rearrange("(a t r) -> t a r", t=4, r=4))
+        nc.scalar.dma_start(out=const_rows[4:4 + TILES, :], in_=inv_spread.rearrange("(i p) -> i p", p=P))
+        nc.scalar.dma_start(out=const_rows[16:16 + Q // P, :], in_=date_weight.rearrange("(i p) -> i p", p=P))
+        load_prior_scales(nc.scalar, 0)
+        nc.scalar.activation(out=warm[:, 4:5], in_=warm[:, 0:1], func=ACT.Tanh)
+        for q in range(1, 4):
+            load_prior_scales(nc.gpsimd, q)
+
+        turn_consts(0)
+        load_series(0)
+        load_wf(3)
+        copy_consts()
+        load_prior_words()
+        turn_x(0, 1, 1)
+        group_wf(0, 0, "vector")
+        turn_x(0, 0, 2)
+        group_wf(0, 1, "vector")
+        load_wf(1)
+        group_wf(3, 1, "vector")
+        spread_weight(2, 3)
+        spread_weight(0, 4)
+        load_series(1)
+        copy_x(0, 0, "vector")
+        copy_weight(2, "vector")
+        turn_x(1, 0, 5)
+        copy_x(0, 1, "scalar")
+        quant_wf(0)
+        group_wf(3, 0, "scalar")
+        group_wf(1, 1, "scalar")
+        load_site(0)
+        quant_series(0)
+        turn_x(1, 1, 6)
+        turn_x(0, 2, 7)
+        load_wf(2)
+        order_prior()
+        group_wf(1, 0, "vector")
+        copy_x(1, 0, "scalar")
+        load_site(1)
+        copy_weight(0, "scalar")
+        quant_wf(1)
+        spread_weight(1, 0)
+        load_series(2)
+        copy_x(1, 1, "scalar")
+        quant_wf(3)
+        group_wf(2, 0, "scalar")
+        group_wf(2, 1, "vector")
+        copy_x(0, 2, "scalar")
+        turn_x(1, 2, 1)
+        copy_x(1, 2, "scalar")
+        quant_series(1)
+        turn_x(2, 1, 2)
+        quant_wf(2)
+        quant_site(0)
+        load_wh(1, 3)
+        copy_weight(1, "scalar")
+        load_wh(0, 1)
+        load_site(2)
+        turn_x(2, 0, 3)
+        copy_x(2, 0, "vector")
+        quant_site(1)
+        load_series(3)
+        copy_x(2, 1, "scalar")
+        stage1(0, 5)
+        stage1(1, 4)
+        turn_x(3, 0, 6)
+        group_wh(2, 1, "scalar")
+        quant_series(2)
+        load_site(3)
+        turn_x(2, 2, 7)
+        group_wh(0, 1, "scalar")
+        group_wh(2, 0, "vector")
+        shrink_coef(0)
+        group_wh(0, 0, "scalar")
+        quant_coef(0)
+        group_wh(1, 0, "scalar")
+        quant_wh(2)
+        group_wh(1, 1, "vector")
+        turn_x(3, 2, 1)
+        load_held(0)
+        shrink_coef(1)
+        quant_wh(0)
+        quant_coef(1)
+        curve(0, 0, 0)
+        copy_x(2, 2, "scalar")
+        quant_wh(1)
+        load_series(4)
+        curve(0, 2, 2)
+        copy_x(3, 0, "scalar")
+        subtract(0, 0)
+        curve(1, 0, 3)
+        curve(0, 1, 5)
+        subtract(0, 2)
+        subtract(0, 1)
+        curve(1, 1, 4)
+        bound(0, 0)
+        load_site(4)
+        load_site(5)
+        curve(1, 2, 7)
+        quant_site(2)
+        turn_x(4, 2, 6)
+        bound(0, 2)
+        bound(0, 1)
+        turn_x(3, 1, 0)
+        load_held(1)
+        subtract(1, 0)
+        copy_x(3, 1, "scalar")
+        bound(1, 0)
+        stage1(2, 2)
+        weigh(0, 0)
+        round_y(0, 0, "scalar")
+        weigh(0, 2)
+        weigh(0, 1)
+        round_y(0, 2, "scalar")
+        subtract(1, 1)
+        load_held(2)
+        load_series(5)
+        turn_y(0, 2, 3, 5)
+        round_y(0, 1, "scalar")
+        load_series(6)
+        shrink_coef(2)
+        weigh(1, 0)
+        load_held(3)
+        turn_y(0, 0, 2, 3)
+        copy_x(3, 2, "scalar")
+        quant_coef(2)
+        turn_x(4, 0, 0)
+        curve(2, 0, 4)
+        quant_series(3)
+        load_site(6)
+        store_y(0, 0, 3)
+        bound(1, 1)
+        quant_site(3)
+        load_held(4)
+        copy_y(0, 0, 2, "scalar")
+        subtract(1, 2)
+        copy_x(4, 0, "scalar")
+        subtract(2, 0)
+        quant_y(0, 0)
+        copy_y(0, 2, 3, "scalar")
+        bound(1, 2)
+        curve(2, 1, 2)
+        weigh(1, 1)
+        round_y(1, 0, "scalar")
+        weigh(1, 2)
+        curve(2, 2, 1)
+        turn_x(4, 1, 3)
+        copy_x(4, 1, "scalar")
+        store_y(1, 0, 3)
+        stage1(3, 7)
+        quant_y(0, 1)
+        subtract(2, 1)
+        copy_x(4, 2, "scalar")
+        subtract(2, 2)
+        round_y(1, 2, "vector")
+        bound(2, 0)
+        quant_y(0, 2)
+        round_y(1, 1, "scalar")
+        quant_series(4)
+        quant_site(4)
+        bound(2, 2)
+        bound(2, 1)
+        load_series(7)
+        load_site(7)
+        load_held(5)
+        shrink_coef(3)
+        turn_x(5, 0, 0)
+        copy_x(5, 0, "scalar")
+        turn_x(5, 1, 1)
+        copy_x(5, 1, "scalar")
+        turn_x(5, 2, 2)
+        copy_x(5, 2, "scalar")
+        weigh(2, 0)
+        quant_coef(3)
+        weigh(2, 1)
+        weigh(2, 2)
+        store_y(2, 0, 3)
+        turn_y(1, 0, 2, 3)
+        copy_y(1, 0, 2, "scalar")
+        turn_y(1, 2, 3, 4)
+        copy_y(1, 2, 3, "scalar")
+        curve(3, 0, 5)
+        subtract(3, 0)
+        bound(3, 0)
+        curve(3, 1, 6)
+        subtract(3, 1)
+        bound(3, 1)
+        curve(3, 2, 0)
+        subtract(3, 2)
+        bound(3, 2)
+        stage1(4, 7)
+        round_y(2, 0, "scalar")
+        round_y(2, 1, "scalar")
+        round_y(2, 2, "scalar")
+        quant_series(5)
+        quant_site(5)
+        quant_y(1, 0)
+        quant_y(1, 1)
+        quant_y(1, 2)
+        load_series(8)
+        load_site(8)
+        load_held(6)
+        shrink_coef(4)
+        turn_x(6, 0, 0)
+        copy_x(6, 0, "scalar")
+        turn_x(6, 1, 1)
+        copy_x(6, 1, "scalar")
+        turn_x(6, 2, 2)
+        copy_x(6, 2, "scalar")
+        weigh(3, 0)
+        quant_coef(4)
+        weigh(3, 1)
+        weigh(3, 2)
+        store_y(3, 0, 3)
+        turn_y(2, 0, 2, 3)
+        copy_y(2, 0, 2, "scalar")
+        turn_y(2, 2, 3, 4)
+        copy_y(2, 2, 3, "scalar")
+        curve(4, 0, 5)
+        subtract(4, 0)
+        bound(4, 0)
+        curve(4, 1, 6)
+        subtract(4, 1)
+        bound(4, 1)
+        curve(4, 2, 0)
+        subtract(4, 2)
+        bound(4, 2)
+        stage1(5, 7)
+        round_y(3, 0, "scalar")
+        round_y(3, 1, "scalar")
+        round_y(3, 2, "vector")
+        quant_series(6)
+        quant_site(6)
+        quant_y(2, 0)
+        quant_y(2, 1)
+        quant_y(2, 2)
+        load_series(9)
+        load_site(9)
+        load_held(7)
+        shrink_coef(5)
+        turn_x(7, 0, 0)
+        copy_x(7, 0, "scalar")
+        turn_x(7, 1, 1)
+        copy_x(7, 1, "scalar")
+        turn_x(7, 2, 2)
+        copy_x(7, 2, "scalar")
+        weigh(4, 0)
+        quant_coef(5)
+        weigh(4, 1)
+        weigh(4, 2)
+        store_y(4, 0, 3)
+        turn_y(3, 0, 2, 3)
+        copy_y(3, 0, 2, "scalar")
+        turn_y(3, 2, 3, 4)
+        copy_y(3, 2, 3, "scalar")
+        curve(5, 0, 5)
+        subtract(5, 0)
+        bound(5, 0)
+        curve(5, 1, 6)
+        subtract(5, 1)
+        bound(5, 1)
+        curve(5, 2, 0)
+        subtract(5, 2)
+        bound(5, 2)
+        stage1(6, 7)
+        round_y(4, 0, "scalar")
+        round_y(4, 1, "scalar")
+        round_y(4, 2, "vector")
+        quant_series(7)
+        quant_site(7)
+        quant_y(3, 0)
+        quant_y(3, 1)
+        quant_y(3, 2)
+        store_codes(0, 4)
+        load_held(8)
+        shrink_coef(6)
+        turn_x(8, 0, 0)
+        copy_x(8, 0, "scalar")
+        turn_x(8, 1, 1)
+        copy_x(8, 1, "scalar")
+        turn_x(8, 2, 2)
+        copy_x(8, 2, "scalar")
+        weigh(5, 0)
+        quant_coef(6)
+        weigh(5, 1)
+        weigh(5, 2)
+        store_y(5, 0, 3)
+        turn_y(4, 0, 2, 3)
+        copy_y(4, 0, 2, "scalar")
+        turn_y(4, 2, 3, 4)
+        copy_y(4, 2, 3, "scalar")
+        curve(6, 0, 5)
+        subtract(6, 0)
+        bound(6, 0)
+        curve(6, 1, 6)
+        subtract(6, 1)
+        bound(6, 1)
+        curve(6, 2, 0)
+        subtract(6, 2)
+        bound(6, 2)
+        stage1(7, 7)
+        round_y(5, 0, "scalar")
+        round_y(5, 1, "scalar")
+        round_y(5, 2, "scalar")
+        quant_series(8)
+        quant_site(8)
+        quant_y(4, 0)
+        quant_y(4, 1)
+        quant_y(4, 2)
+        load_held(9)
+        shrink_coef(7)
+        turn_x(9, 0, 0)
+        copy_x(9, 0, "scalar")
+        turn_x(9, 1, 1)
+        copy_x(9, 1, "scalar")
+        turn_x(9, 2, 2)
+        copy_x(9, 2, "scalar")
+        weigh(6, 0)
+        quant_coef(7)
+        weigh(6, 1)
+        weigh(6, 2)
+        store_y(6, 0, 3)
+        turn_y(5, 0, 2, 3)
+        copy_y(5, 0, 2, "scalar")
+        turn_y(5, 2, 3, 4)
+        copy_y(5, 2, 3, "scalar")
+        curve(7, 0, 5)
+        subtract(7, 0)
+        bound(7, 0)
+        curve(7, 1, 6)
+        subtract(7, 1)
+        bound(7, 1)
+        curve(7, 2, 0)
+        subtract(7, 2)
+        bound(7, 2)
+        stage1(8, 7)
+        round_y(6, 0, "scalar")
+        round_y(6, 1, "scalar")
+        round_y(6, 2, "vector")
+        quant_series(9)
+        quant_site(9)
+        quant_y(5, 0)
+        quant_y(5, 1)
+        quant_y(5, 2)
+        shrink_coef(8)
+        weigh(7, 0)
+        round_y(7, 0, "scalar")
+        turn_y(6, 2, 3, 1)
+        quant_coef(8)
+        stage1(9, 2)
+        weigh(7, 1)
+        weigh(7, 2)
+        curve(8, 0, 5)
+        shrink_coef(9)
+        subtract(8, 0)
+        round_y(7, 1, "scalar")
+        curve(8, 1, 3)
+        store_y(7, 0, 3)
+        round_y(7, 2, "scalar")
+        turn_y(6, 0, 2, 6)
+        curve(8, 2, 4)
+        quant_coef(9)
+        copy_y(6, 0, 2, "scalar")
+        subtract(8, 1)
+        turn_y(7, 2, 3, 0)
+        turn_y(7, 0, 2, 7)
+        bound(8, 0)
+        curve(9, 0, 2)
+        bound(8, 1)
+        subtract(8, 2)
+        subtract(9, 0)
+        curve(9, 2, 5)
+        weigh(8, 0)
+        bound(8, 2)
+        weigh(8, 2)
+        weigh(8, 1)
+        copy_y(7, 0, 2, "scalar")
+        bound(9, 0)
+        copy_y(7, 2, 3, "scalar")
+        round_y(8, 0, "scalar")
+        quant_y(7, 1)
+        copy_y(6, 2, 3, "scalar")
+        quant_y(6, 1)
+        round_y(8, 1, "scalar")
+        quant_y(6, 0)
+        quant_y(7, 0)
+        curve(9, 1, 6)
+        subtract(9, 2)
+        weigh(9, 0)
+        bound(9, 2)
+        round_y(9, 0, "scalar")
+        quant_y(6, 2)
+        quant_y(7, 2)
+        subtract(9, 1)
+        bound(9, 1)
+        weigh(9, 2)
+        turn_y(8, 0, 2, 3)
+        turn_y(9, 0, 1, 4)
+        round_y(9, 2, "scalar")
+        copy_y(8, 0, 2, "scalar")
+        round_y(8, 2, "vector")
+        turn_y(8, 2, 3, 2)
+        store_y(8, 0, 3)
+        weigh(9, 1)
+        copy_y(9, 0, 1, "scalar")
+        round_y(9, 1, "vector")
+        copy_y(8, 2, 3, "vector")
+        store_y(9, 0, 1)
+        quant_y(8, 0)
+        quant_y(9, 0)
+        turn_y(9, 2, 3, 7)
+        turn_y(9, 1, 2, 0)
+        quant_y(8, 2)
+        copy_y(9, 2, 3, "scalar")
+        store_scales(0, 8)
+        copy_y(9, 1, 2, "scalar")
+        store_codes(4, 8)
+        store_y(9, 2, 3)
+        quant_y(8, 1)
+        store_y(9, 1, 2)
+        quant_y(9, 2)
+        quant_y(9, 1)
+        store_codes(8, 10)
+        store_scales(8, 10)

@@ -33,9 +33,19 @@ def tile_harmonic_phenology_anomaly_k6_kernel(
         psum = ctx.enter_context(tc.psum_pool(name="psum", bufs=1))
         ctx.enter_context(tc.manual_schedule())
 
-        def bank(k, dtype=F32):
+        t = {}
+        free_banks = list(range(8))
+        bank_of = {}
+
+        def take_bank(key, dtype=F32):
+            k = free_banks.pop(0)
+            bank_of[key] = k
             width = 512 if dtype == F32 else 1024
-            return psum.tile([P, width], dtype, name="bank%d" % k, tag="bank%d" % k)
+            t[key] = psum.tile([P, width], dtype, name="bank%d" % k, tag="bank%d" % k)
+            return t[key]
+
+        def give_bank(key):
+            free_banks.append(bank_of[key])
 
         ident = keep.tile([P, P], F32, name="ident")
         ident_bf = keep.tile([P, P], BF16, name="ident_bf")
@@ -58,7 +68,6 @@ def tile_harmonic_phenology_anomaly_k6_kernel(
         y_scales = keep.tile([P, GQ, NPIX], U8, name="y_scales", align_bytes=64)
         w_grouped = keep.tile([P, GT + GQ, 4 * KP], BF16, name="w_grouped", align_bytes=64)
 
-        t = {}
 
         def px(i):
             return slice(i * P, (i + 1) * P)
@@ -125,12 +134,11 @@ def tile_harmonic_phenology_anomaly_k6_kernel(
                 out=ps[:].bitcast(I32).rearrange("p g (t a) -> p g t a", t=4),
                 in_=ps_raw[:].bitcast(I32).rearrange("p g (a t) -> p g t a", t=4))
 
-        def turn_x(i, b, k):
+        def turn_x(i, b):
             src = t["series", i] if b < 2 else t["site", i]
             words = src[:].bitcast(F32)
             g0 = 2 * b if b < 2 else 0
-            pt = bank(k)
-            t["xt", i, b] = pt
+            pt = take_bank(("xt", i, b))
             for gg in range(2):
                 for u in range(2):
                     lo = 256 * (g0 + gg)
@@ -139,11 +147,12 @@ def tile_harmonic_phenology_anomaly_k6_kernel(
 
         def copy_x(i, b, engine):
             if b == 0:
-                t["xg", i] = work.tile([P, T + D], BF16, name="xg", align_bytes=64)
+                t["xg", i] = work.tile([P, T + D], BF16, name="xg", align_bytes=64, bufs=3)
             xg_words = t["xg", i][:].bitcast(F32)
             copy_on(engine,
                     xg_words[:, 512 * b:512 * (b + 1)].rearrange("p (g m u) -> p g m u", g=2, u=2),
                     t["xt", i, b][:].rearrange("p (g u m) -> p g m u", g=2, u=2))
+            give_bank(("xt", i, b))
 
         def x_tiles(i):
             if ("xc", i) not in t:
@@ -158,9 +167,8 @@ def tile_harmonic_phenology_anomaly_k6_kernel(
             x_tiles(i)
             nc.vector.quantize_mx(out=t["xc", i][:, GT * P:].bitcast(FP8X4), scales=t["xs", i][:, GT * P:], in_=t["xg", i][:, T:])
 
-        def stage1(i, k):
-            acc = bank(k)
-            t["acc", i] = acc
+        def stage1(i):
+            acc = take_bank(("acc", i))
             xc, xs = t["xc", i], t["xs", i]
             for s in range(4):
                 for g in range(GT + GD):
@@ -180,14 +188,15 @@ def tile_harmonic_phenology_anomaly_k6_kernel(
                 in0=t["acc", i][:].rearrange("p (s m) -> p m s", s=4),
                 in1=const_cols[:, 0:4].unsqueeze(1).to_broadcast([P, P, 4]),
                 op=ALU.mult)
+            give_bank(("acc", i))
 
         def quant_coef(i):
             t["cc", i] = work.tile([P, P], U32, name="cc", align_bytes=64, bufs=3)
             t["cs", i] = work.tile([P, P], U8, name="cs", align_bytes=64, bufs=3)
             nc.vector.quantize_mx(out=t["cc", i][:].bitcast(FP8X4), scales=t["cs", i][:], in_=t["coef", i][:])
 
-        def curve(i, g, k):
-            t["curve", i, g] = bank(k)
+        def curve(i, g):
+            take_bank(("curve", i, g))
             nc.tensor.matmul_mx(out=t["curve", i, g][:], lhsT=t["cc", i][:].bitcast(FP8X4), lhsT_scale=t["cs", i][:],
                                 rhs=wh_codes[:, grp(g)].bitcast(FP8X4), rhs_scale=wh_scales[:, grp(g)],
                                 start=True, stop=True)
@@ -196,35 +205,39 @@ def tile_harmonic_phenology_anomaly_k6_kernel(
             if g == 0:
                 t["diff", i] = work.tile([P, Q], F32, name="diff")
             nc.vector.tensor_tensor(out=t["diff", i][:, grp(g)], in0=t["held", i][:, grp(g)], in1=t["curve", i, g][:], op=ALU.subtract)
+            give_bank(("curve", i, g))
 
-        def bound(i, g):
-            if g == 0:
+        def bound(i, g0, g1):
+            if g0 == 0:
                 t["tanh", i] = work.tile([P, Q], F32, name="tanh")
-            nc.scalar.activation(out=t["tanh", i][:, grp(g)], in_=t["diff", i][:, grp(g)], func=ACT.Tanh,
+            cols = slice(g0 * KP, g1 * KP)
+            nc.scalar.activation(out=t["tanh", i][:, cols], in_=t["diff", i][:, cols], func=ACT.Tanh,
                                  scale=const_cols[:, 4 + i:5 + i])
 
-        def weigh(i, g, engine=nc.vector):
-            if g == 0:
+        def weigh(i, g0, g1):
+            if g0 == 0:
                 t["y", i] = work.tile([P, Q], F32, name="y", bufs=3)
-            engine.tensor_tensor(out=t["y", i][:, grp(g)], in0=t["tanh", i][:, grp(g)], in1=weight_bc[:, grp(g)], op=ALU.mult)
+            cols = slice(g0 * KP, g1 * KP)
+            nc.vector.tensor_tensor(out=t["y", i][:, cols], in0=t["tanh", i][:, cols], in1=weight_bc[:, cols], op=ALU.mult)
 
         def store_y(i, g0, g1):
             cols = slice(g0 * KP, g1 * KP)
             nc.sync.dma_start(out=out_0[px(i), cols], in_=t["y", i][:, cols])
 
-        def round_y(i, g, engine):
-            if g == 0:
+        def round_y(i, g0, g1, engine):
+            if g0 == 0:
                 t["yb", i] = work.tile([P, Q], BF16, name="yb")
+            pairs = slice(g0 * P, g1 * P)
             copy_on(engine,
-                    t["yb", i][:, grp(g)].rearrange("m (u p e) -> m u p e", u=2, e=2),
-                    t["y", i][:, grp(g)].rearrange("m (p u e) -> m u p e", u=2, e=2))
+                    t["yb", i][:].rearrange("m (u c e) -> m u c e", u=2, e=2)[:, :, pairs, :],
+                    t["y", i][:].rearrange("m (c u e) -> m u c e", u=2, e=2)[:, :, pairs, :])
 
-        def turn_y(i, g0, g1, k):
+        def turn_y(i, g0, g1):
             words = t["yb", i][:].bitcast(F32)
-            pt = bank(k)
-            t["ytp", i, g0] = pt
-            for j in range(2 * g0, 2 * g1):
-                nc.tensor.transpose(pt[:, px(j - 2 * g0)], words[:, px(j)], ident[:])
+            pt = take_bank(("ytp", i, g0))
+            for g in range(g0, g1):
+                for u in range(2):
+                    nc.tensor.transpose(pt[:, px(2 * (g - g0) + u)], words[:, px(GQ * u + g)], ident[:])
 
         def copy_y(i, g0, g1, engine):
             if g0 == 0:
@@ -233,25 +246,28 @@ def tile_harmonic_phenology_anomaly_k6_kernel(
             copy_on(engine,
                     yt_words[:, 2 * g0 * P:2 * g1 * P].rearrange("p (g m u) -> p g m u", m=P, u=2),
                     t["ytp", i, g0][:, 0:2 * (g1 - g0) * P].rearrange("p (g u m) -> p g m u", m=P, u=2))
+            give_bank(("ytp", i, g0))
 
         def quant_y(i, g):
             nc.vector.quantize_mx(out=y_codes[:, g, px(i)].bitcast(FP8X4), scales=y_scales[:, g, px(i)], in_=t["yt", i][:, grp(g)])
 
-        def turn_consts(k):
-            t["consts"] = bank(k, BF16)
+        def turn_consts():
+            take_bank("consts", BF16)
             nc.tensor.transpose(t["consts"][:, 0:P], const_rows[:], ident_bf[:])
 
         def copy_consts():
             nc.scalar.copy(out=weight_cols[:], in_=t["consts"][:, 16:32])
             nc.scalar.copy(out=const_cols[:], in_=t["consts"][:, 0:16])
+            give_bank("consts")
 
-        def spread_weight(g, k):
-            t["wt", g] = bank(k, BF16)
+        def spread_weight(g):
+            take_bank(("wt", g), BF16)
             for c in range(4):
                 nc.tensor.transpose(t["wt", g][:, px(c)], weight_cols[:, 4 * g + c:4 * g + c + 1].to_broadcast([P, P]), ident_bf[:])
 
         def copy_weight(g, engine):
             copy_on(engine, weight_bc[:, grp(g)], t["wt", g][:, 0:KP])
+            give_bank(("wt", g))
 
         def store_codes(i0, i1):
             cols = slice(i0 * P, i1 * P)
@@ -283,418 +299,390 @@ def tile_harmonic_phenology_anomaly_k6_kernel(
         for q in range(1, 4):
             load_prior_scales(nc.gpsimd, q)
 
-        turn_consts(0)
-        load_series(0)
-        load_wf(3)
+        turn_consts()
         copy_consts()
-        load_prior_words()
-        turn_x(0, 1, 1)
-        group_wf(0, 0, "vector")
-        turn_x(0, 0, 2)
-        group_wf(0, 1, "vector")
         load_wf(1)
-        group_wf(3, 1, "vector")
-        spread_weight(2, 3)
-        spread_weight(0, 4)
-        load_series(1)
-        copy_x(0, 0, "vector")
-        copy_weight(2, "vector")
-        turn_x(1, 0, 5)
-        copy_x(0, 1, "scalar")
-        quant_wf(0)
-        group_wf(3, 0, "scalar")
-        group_wf(1, 1, "scalar")
-        load_site(0)
-        quant_series(0)
-        turn_x(1, 1, 6)
-        turn_x(0, 2, 7)
         load_wf(2)
-        order_prior()
+        group_wf(0, 0, "scalar")
+        load_series(0)
+        load_series(1)
+        spread_weight(1)
+        load_wf(3)
+        load_site(0)
+        group_wf(0, 1, "vector")
+        turn_x(0, 0)
         group_wf(1, 0, "vector")
-        copy_x(1, 0, "scalar")
+        group_wf(2, 1, "vector")
+        turn_x(0, 1)
+        group_wf(2, 0, "vector")
+        spread_weight(0)
         load_site(1)
-        copy_weight(0, "scalar")
-        quant_wf(1)
-        spread_weight(1, 0)
+        quant_wf(0)
+        copy_x(0, 0, "vector")
         load_series(2)
+        turn_x(1, 0)
+        group_wf(1, 1, "scalar")
+        load_series(3)
+        copy_x(0, 1, "vector")
+        turn_x(1, 1)
+        spread_weight(2)
+        load_prior_words()
+        copy_x(1, 0, "scalar")
+        quant_wf(2)
+        load_wh(1, 3)
+        group_wf(3, 0, "scalar")
+        quant_series(0)
+        turn_x(0, 2)
+        turn_x(1, 2)
+        load_wh(0, 1)
+        load_series(4)
+        copy_weight(1, "scalar")
+        group_wf(3, 1, "vector")
+        copy_x(0, 2, "scalar")
+        copy_x(1, 2, "vector")
+        load_site(2)
         copy_x(1, 1, "scalar")
         quant_wf(3)
-        group_wf(2, 0, "scalar")
-        group_wf(2, 1, "vector")
-        copy_x(0, 2, "scalar")
-        turn_x(1, 2, 1)
-        copy_x(1, 2, "scalar")
-        quant_series(1)
-        turn_x(2, 1, 2)
-        quant_wf(2)
-        quant_site(0)
-        load_wh(1, 3)
-        copy_weight(1, "scalar")
-        load_wh(0, 1)
-        load_site(2)
-        turn_x(2, 0, 3)
-        copy_x(2, 0, "vector")
-        quant_site(1)
-        load_series(3)
-        copy_x(2, 1, "scalar")
-        stage1(0, 5)
-        stage1(1, 4)
-        turn_x(3, 0, 6)
-        group_wh(2, 1, "scalar")
-        quant_series(2)
-        load_site(3)
-        turn_x(2, 2, 7)
-        group_wh(0, 1, "scalar")
-        group_wh(2, 0, "vector")
-        shrink_coef(0)
-        group_wh(0, 0, "scalar")
-        quant_coef(0)
-        group_wh(1, 0, "scalar")
-        quant_wh(2)
-        group_wh(1, 1, "vector")
-        turn_x(3, 2, 1)
+        copy_weight(0, "scalar")
+        quant_wf(1)
+        turn_x(2, 0)
+        turn_x(2, 1)
         load_held(0)
-        shrink_coef(1)
-        quant_wh(0)
-        quant_coef(1)
-        curve(0, 0, 0)
-        copy_x(2, 2, "scalar")
-        quant_wh(1)
-        load_series(4)
-        curve(0, 2, 2)
+        quant_site(0)
+        copy_weight(2, "scalar")
+        order_prior()
+        copy_x(2, 0, "scalar")
+        load_site(3)
+        load_site(4)
+        turn_x(3, 1)
+        quant_series(1)
+        copy_x(2, 1, "scalar")
+        quant_site(1)
+        load_series(5)
+        quant_series(2)
+        turn_x(3, 0)
+        stage1(0)
+        group_wh(1, 1, "vector")
+        stage1(1)
+        group_wh(2, 1, "vector")
+        group_wh(0, 1, "vector")
+        turn_x(4, 1)
+        turn_x(4, 0)
+        group_wh(1, 0, "scalar")
+        group_wh(0, 0, "scalar")
         copy_x(3, 0, "scalar")
+        shrink_coef(0)
+        quant_wh(1)
+        group_wh(2, 0, "scalar")
+        quant_wh(0)
+        turn_x(2, 2)
+        shrink_coef(1)
+        quant_coef(0)
+        quant_wh(2)
+        curve(0, 0)
+        copy_x(3, 1, "scalar")
+        curve(0, 1)
+        copy_x(4, 0, "scalar")
+        copy_x(2, 2, "scalar")
+        load_held(1)
+        quant_series(3)
+        quant_coef(1)
+        curve(0, 2)
+        turn_x(3, 2)
+        curve(1, 2)
+        curve(1, 0)
         subtract(0, 0)
-        curve(1, 0, 3)
-        curve(0, 1, 5)
+        copy_x(4, 1, "scalar")
+        load_site(5)
         subtract(0, 2)
         subtract(0, 1)
-        curve(1, 1, 4)
-        bound(0, 0)
-        load_site(4)
-        load_site(5)
-        curve(1, 2, 7)
-        quant_site(2)
-        turn_x(4, 2, 6)
-        bound(0, 2)
-        bound(0, 1)
-        turn_x(3, 1, 0)
-        load_held(1)
+        curve(1, 1)
+        bound(0, 0, 1)
         subtract(1, 0)
-        copy_x(3, 1, "scalar")
-        bound(1, 0)
-        stage1(2, 2)
-        weigh(0, 0)
-        round_y(0, 0, "scalar")
-        weigh(0, 2)
-        weigh(0, 1)
-        round_y(0, 2, "scalar")
-        subtract(1, 1)
-        load_held(2)
-        load_series(5)
-        turn_y(0, 2, 3, 5)
-        round_y(0, 1, "scalar")
-        load_series(6)
-        shrink_coef(2)
-        weigh(1, 0)
-        load_held(3)
-        turn_y(0, 0, 2, 3)
+        turn_x(4, 2)
+        quant_site(2)
         copy_x(3, 2, "scalar")
-        quant_coef(2)
-        turn_x(4, 0, 0)
-        curve(2, 0, 4)
-        quant_series(3)
-        load_site(6)
-        store_y(0, 0, 3)
-        bound(1, 1)
         quant_site(3)
-        load_held(4)
-        copy_y(0, 0, 2, "scalar")
+        bound(0, 1, 2)
+        turn_x(5, 0)
         subtract(1, 2)
-        copy_x(4, 0, "scalar")
-        subtract(2, 0)
-        quant_y(0, 0)
-        copy_y(0, 2, 3, "scalar")
-        bound(1, 2)
-        curve(2, 1, 2)
-        weigh(1, 1)
-        round_y(1, 0, "scalar")
-        weigh(1, 2)
-        curve(2, 2, 1)
-        turn_x(4, 1, 3)
-        copy_x(4, 1, "scalar")
-        store_y(1, 0, 3)
-        stage1(3, 7)
-        quant_y(0, 1)
-        subtract(2, 1)
+        bound(0, 2, 3)
+        load_held(2)
+        turn_x(5, 2)
+        subtract(1, 1)
+        stage1(2)
+        bound(1, 0, 1)
+        load_site(6)
+        copy_x(5, 0, "scalar")
+        stage1(3)
+        bound(1, 2, 3)
         copy_x(4, 2, "scalar")
-        subtract(2, 2)
-        round_y(1, 2, "vector")
-        bound(2, 0)
-        quant_y(0, 2)
-        round_y(1, 1, "scalar")
+        bound(1, 1, 2)
+        weigh(0, 0, 3)
+        shrink_coef(2)
+        round_y(0, 0, 3, "scalar")
+        copy_x(5, 2, "scalar")
+        load_series(6)
         quant_series(4)
         quant_site(4)
-        bound(2, 2)
-        bound(2, 1)
+        quant_coef(2)
+        turn_x(5, 1)
+        weigh(1, 0, 3)
+        turn_y(0, 0, 2)
+        turn_y(0, 2, 3)
+        copy_x(5, 1, "scalar")
+        curve(2, 0)
+        copy_y(0, 0, 2, "scalar")
+        curve(2, 2)
+        load_held(3)
+        copy_y(0, 2, 3, "scalar")
+        round_y(1, 0, 3, "gpsimd")
+        store_y(0, 0, 3)
+        curve(2, 1)
+        store_y(1, 0, 3)
         load_series(7)
         load_site(7)
-        load_held(5)
+        load_held(4)
+        turn_x(6, 0)
+        turn_x(6, 1)
+        subtract(2, 0)
+        bound(2, 0, 1)
+        subtract(2, 1)
+        copy_x(6, 0, "scalar")
+        subtract(2, 2)
+        bound(2, 1, 2)
+        stage1(4)
         shrink_coef(3)
-        turn_x(5, 0, 0)
-        copy_x(5, 0, "scalar")
-        turn_x(5, 1, 1)
-        copy_x(5, 1, "scalar")
-        turn_x(5, 2, 2)
-        copy_x(5, 2, "scalar")
-        weigh(2, 0)
+        copy_x(6, 1, "scalar")
+        bound(2, 2, 3)
+        quant_y(0, 0)
+        quant_y(0, 1)
+        quant_y(0, 2)
         quant_coef(3)
-        weigh(2, 1)
-        weigh(2, 2)
-        store_y(2, 0, 3)
-        turn_y(1, 0, 2, 3)
-        copy_y(1, 0, 2, "scalar")
-        turn_y(1, 2, 3, 4)
-        copy_y(1, 2, 3, "scalar")
-        curve(3, 0, 5)
-        subtract(3, 0)
-        bound(3, 0)
-        curve(3, 1, 6)
-        subtract(3, 1)
-        bound(3, 1)
-        curve(3, 2, 0)
-        subtract(3, 2)
-        bound(3, 2)
-        stage1(4, 7)
-        round_y(2, 0, "scalar")
-        round_y(2, 1, "scalar")
-        round_y(2, 2, "scalar")
+        turn_x(6, 2)
+        turn_y(1, 0, 2)
+        turn_y(1, 2, 3)
         quant_series(5)
         quant_site(5)
+        copy_x(6, 2, "scalar")
+        copy_y(1, 0, 2, "scalar")
+        copy_y(1, 2, 3, "scalar")
+        curve(3, 0)
+        curve(3, 1)
+        curve(3, 2)
+        weigh(2, 0, 3)
+        store_y(2, 0, 3)
+        round_y(2, 0, 3, "gpsimd")
+        load_series(8)
+        load_site(8)
+        load_held(5)
+        turn_x(7, 0)
+        turn_x(7, 1)
+        subtract(3, 0)
+        bound(3, 0, 1)
+        subtract(3, 1)
+        copy_x(7, 0, "scalar")
+        subtract(3, 2)
+        bound(3, 1, 2)
+        stage1(5)
+        shrink_coef(4)
+        copy_x(7, 1, "scalar")
+        bound(3, 2, 3)
         quant_y(1, 0)
         quant_y(1, 1)
         quant_y(1, 2)
-        load_series(8)
-        load_site(8)
-        load_held(6)
-        shrink_coef(4)
-        turn_x(6, 0, 0)
-        copy_x(6, 0, "scalar")
-        turn_x(6, 1, 1)
-        copy_x(6, 1, "scalar")
-        turn_x(6, 2, 2)
-        copy_x(6, 2, "scalar")
-        weigh(3, 0)
         quant_coef(4)
-        weigh(3, 1)
-        weigh(3, 2)
-        store_y(3, 0, 3)
-        turn_y(2, 0, 2, 3)
-        copy_y(2, 0, 2, "scalar")
-        turn_y(2, 2, 3, 4)
-        copy_y(2, 2, 3, "scalar")
-        curve(4, 0, 5)
-        subtract(4, 0)
-        bound(4, 0)
-        curve(4, 1, 6)
-        subtract(4, 1)
-        bound(4, 1)
-        curve(4, 2, 0)
-        subtract(4, 2)
-        bound(4, 2)
-        stage1(5, 7)
-        round_y(3, 0, "scalar")
-        round_y(3, 1, "scalar")
-        round_y(3, 2, "vector")
+        turn_x(7, 2)
+        turn_y(2, 0, 2)
+        turn_y(2, 2, 3)
         quant_series(6)
         quant_site(6)
+        copy_x(7, 2, "scalar")
+        copy_y(2, 0, 2, "scalar")
+        copy_y(2, 2, 3, "scalar")
+        curve(4, 0)
+        curve(4, 1)
+        curve(4, 2)
+        weigh(3, 0, 3)
+        store_y(3, 0, 3)
+        round_y(3, 0, 3, "gpsimd")
+        load_series(9)
+        load_site(9)
+        load_held(6)
+        turn_x(8, 0)
+        turn_x(8, 1)
+        subtract(4, 0)
+        bound(4, 0, 1)
+        subtract(4, 1)
+        copy_x(8, 0, "scalar")
+        subtract(4, 2)
+        bound(4, 1, 2)
+        stage1(6)
+        shrink_coef(5)
+        copy_x(8, 1, "scalar")
+        bound(4, 2, 3)
         quant_y(2, 0)
         quant_y(2, 1)
         quant_y(2, 2)
-        load_series(9)
-        load_site(9)
-        load_held(7)
-        shrink_coef(5)
-        turn_x(7, 0, 0)
-        copy_x(7, 0, "scalar")
-        turn_x(7, 1, 1)
-        copy_x(7, 1, "scalar")
-        turn_x(7, 2, 2)
-        copy_x(7, 2, "scalar")
-        weigh(4, 0)
         quant_coef(5)
-        weigh(4, 1)
-        weigh(4, 2)
-        store_y(4, 0, 3)
-        turn_y(3, 0, 2, 3)
-        copy_y(3, 0, 2, "scalar")
-        turn_y(3, 2, 3, 4)
-        copy_y(3, 2, 3, "scalar")
-        curve(5, 0, 5)
-        subtract(5, 0)
-        bound(5, 0)
-        curve(5, 1, 6)
-        subtract(5, 1)
-        bound(5, 1)
-        curve(5, 2, 0)
-        subtract(5, 2)
-        bound(5, 2)
-        stage1(6, 7)
-        round_y(4, 0, "scalar")
-        round_y(4, 1, "scalar")
-        round_y(4, 2, "vector")
+        turn_x(8, 2)
+        turn_y(3, 0, 2)
+        turn_y(3, 2, 3)
         quant_series(7)
         quant_site(7)
+        copy_x(8, 2, "scalar")
+        copy_y(3, 0, 2, "scalar")
+        copy_y(3, 2, 3, "scalar")
+        curve(5, 0)
+        curve(5, 1)
+        curve(5, 2)
+        weigh(4, 0, 3)
+        store_y(4, 0, 3)
+        round_y(4, 0, 3, "gpsimd")
+        load_held(7)
+        turn_x(9, 0)
+        turn_x(9, 1)
+        subtract(5, 0)
+        bound(5, 0, 1)
+        subtract(5, 1)
+        copy_x(9, 0, "scalar")
+        subtract(5, 2)
+        bound(5, 1, 2)
+        stage1(7)
+        shrink_coef(6)
+        copy_x(9, 1, "scalar")
+        bound(5, 2, 3)
         quant_y(3, 0)
         quant_y(3, 1)
         quant_y(3, 2)
         store_codes(0, 4)
-        load_held(8)
-        shrink_coef(6)
-        turn_x(8, 0, 0)
-        copy_x(8, 0, "scalar")
-        turn_x(8, 1, 1)
-        copy_x(8, 1, "scalar")
-        turn_x(8, 2, 2)
-        copy_x(8, 2, "scalar")
-        weigh(5, 0)
         quant_coef(6)
-        weigh(5, 1)
-        weigh(5, 2)
-        store_y(5, 0, 3)
-        turn_y(4, 0, 2, 3)
-        copy_y(4, 0, 2, "scalar")
-        turn_y(4, 2, 3, 4)
-        copy_y(4, 2, 3, "scalar")
-        curve(6, 0, 5)
-        subtract(6, 0)
-        bound(6, 0)
-        curve(6, 1, 6)
-        subtract(6, 1)
-        bound(6, 1)
-        curve(6, 2, 0)
-        subtract(6, 2)
-        bound(6, 2)
-        stage1(7, 7)
-        round_y(5, 0, "scalar")
-        round_y(5, 1, "scalar")
-        round_y(5, 2, "scalar")
+        turn_x(9, 2)
+        turn_y(4, 0, 2)
+        turn_y(4, 2, 3)
         quant_series(8)
         quant_site(8)
+        copy_x(9, 2, "scalar")
+        copy_y(4, 0, 2, "scalar")
+        copy_y(4, 2, 3, "scalar")
+        curve(6, 0)
+        curve(6, 1)
+        curve(6, 2)
+        weigh(5, 0, 3)
+        store_y(5, 0, 3)
+        round_y(5, 0, 3, "gpsimd")
+        load_held(8)
+        subtract(6, 0)
+        bound(6, 0, 1)
+        subtract(6, 1)
+        subtract(6, 2)
+        bound(6, 1, 2)
+        stage1(8)
+        shrink_coef(7)
+        bound(6, 2, 3)
         quant_y(4, 0)
         quant_y(4, 1)
         quant_y(4, 2)
-        load_held(9)
-        shrink_coef(7)
-        turn_x(9, 0, 0)
-        copy_x(9, 0, "scalar")
-        turn_x(9, 1, 1)
-        copy_x(9, 1, "scalar")
-        turn_x(9, 2, 2)
-        copy_x(9, 2, "scalar")
-        weigh(6, 0)
         quant_coef(7)
-        weigh(6, 1)
-        weigh(6, 2)
-        store_y(6, 0, 3)
-        turn_y(5, 0, 2, 3)
-        copy_y(5, 0, 2, "scalar")
-        turn_y(5, 2, 3, 4)
-        copy_y(5, 2, 3, "scalar")
-        curve(7, 0, 5)
-        subtract(7, 0)
-        bound(7, 0)
-        curve(7, 1, 6)
-        subtract(7, 1)
-        bound(7, 1)
-        curve(7, 2, 0)
-        subtract(7, 2)
-        bound(7, 2)
-        stage1(8, 7)
-        round_y(6, 0, "scalar")
-        round_y(6, 1, "scalar")
-        round_y(6, 2, "vector")
+        turn_y(5, 0, 2)
+        turn_y(5, 2, 3)
         quant_series(9)
         quant_site(9)
-        quant_y(5, 0)
-        quant_y(5, 1)
-        quant_y(5, 2)
+        copy_y(5, 0, 2, "scalar")
+        copy_y(5, 2, 3, "scalar")
+        curve(7, 0)
+        curve(7, 1)
+        curve(7, 2)
+        weigh(6, 0, 3)
+        store_y(6, 0, 3)
+        round_y(6, 0, 3, "gpsimd")
         shrink_coef(8)
-        weigh(7, 0)
-        round_y(7, 0, "scalar")
-        turn_y(6, 2, 3, 1)
+        load_held(9)
+        subtract(7, 0)
+        subtract(7, 2)
+        subtract(7, 1)
         quant_coef(8)
-        stage1(9, 2)
-        weigh(7, 1)
-        weigh(7, 2)
-        curve(8, 0, 5)
+        bound(7, 0, 1)
+        stage1(9)
         shrink_coef(9)
-        subtract(8, 0)
-        round_y(7, 1, "scalar")
-        curve(8, 1, 3)
-        store_y(7, 0, 3)
-        round_y(7, 2, "scalar")
-        turn_y(6, 0, 2, 6)
-        curve(8, 2, 4)
-        quant_coef(9)
+        bound(7, 2, 3)
+        turn_y(6, 0, 2)
+        turn_y(6, 2, 3)
+        quant_y(5, 1)
+        quant_y(5, 0)
+        bound(7, 1, 2)
         copy_y(6, 0, 2, "scalar")
-        subtract(8, 1)
-        turn_y(7, 2, 3, 0)
-        turn_y(7, 0, 2, 7)
-        bound(8, 0)
-        curve(9, 0, 2)
-        bound(8, 1)
-        subtract(8, 2)
-        subtract(9, 0)
-        curve(9, 2, 5)
-        weigh(8, 0)
-        bound(8, 2)
-        weigh(8, 2)
-        weigh(8, 1)
-        copy_y(7, 0, 2, "scalar")
-        bound(9, 0)
-        copy_y(7, 2, 3, "scalar")
-        round_y(8, 0, "scalar")
-        quant_y(7, 1)
+        curve(8, 0)
+        quant_coef(9)
+        weigh(7, 0, 3)
+        quant_y(5, 2)
+        subtract(8, 0)
+        round_y(7, 0, 3, "gpsimd")
+        curve(8, 2)
+        store_y(7, 0, 3)
         copy_y(6, 2, 3, "scalar")
-        quant_y(6, 1)
-        round_y(8, 1, "scalar")
-        quant_y(6, 0)
-        quant_y(7, 0)
-        curve(9, 1, 6)
-        subtract(9, 2)
-        weigh(9, 0)
-        bound(9, 2)
-        round_y(9, 0, "scalar")
-        quant_y(6, 2)
-        quant_y(7, 2)
+        curve(9, 0)
+        subtract(9, 0)
+        bound(8, 0, 1)
+        curve(8, 1)
+        curve(9, 2)
+        curve(9, 1)
+        bound(9, 0, 1)
         subtract(9, 1)
-        bound(9, 1)
-        weigh(9, 2)
-        turn_y(8, 0, 2, 3)
-        turn_y(9, 0, 1, 4)
-        round_y(9, 2, "scalar")
-        copy_y(8, 0, 2, "scalar")
-        round_y(8, 2, "vector")
-        turn_y(8, 2, 3, 2)
-        store_y(8, 0, 3)
-        weigh(9, 1)
-        copy_y(9, 0, 1, "scalar")
-        round_y(9, 1, "vector")
-        copy_y(8, 2, 3, "vector")
+        turn_y(7, 0, 2)
+        turn_y(7, 2, 3)
+        bound(9, 1, 2)
+        subtract(9, 2)
+        weigh(8, 0, 1)
+        round_y(8, 0, 1, "gpsimd")
+        bound(9, 2, 3)
+        weigh(9, 0, 1)
+        turn_y(8, 0, 1)
+        copy_y(7, 0, 2, "scalar")
+        subtract(8, 1)
+        copy_y(7, 2, 3, "scalar")
+        round_y(9, 0, 1, "scalar")
+        subtract(8, 2)
+        weigh(9, 1, 2)
+        bound(8, 1, 2)
+        bound(8, 2, 3)
+        weigh(9, 2, 3)
+        weigh(8, 1, 2)
+        store_y(8, 0, 1)
+        weigh(8, 2, 3)
+        quant_y(6, 2)
+        round_y(9, 2, 3, "gpsimd")
+        quant_y(7, 1)
+        round_y(9, 1, 2, "scalar")
         store_y(9, 0, 1)
-        quant_y(8, 0)
-        quant_y(9, 0)
-        turn_y(9, 2, 3, 7)
-        turn_y(9, 1, 2, 0)
-        quant_y(8, 2)
-        copy_y(9, 2, 3, "scalar")
-        store_scales(0, 8)
-        copy_y(9, 1, 2, "scalar")
-        store_codes(4, 8)
-        store_y(9, 2, 3)
-        quant_y(8, 1)
+        round_y(8, 1, 2, "scalar")
+        turn_y(9, 0, 1)
         store_y(9, 1, 2)
-        quant_y(9, 2)
+        quant_y(6, 1)
+        turn_y(9, 1, 2)
+        quant_y(7, 0)
+        quant_y(6, 0)
+        quant_y(7, 2)
+        round_y(8, 2, 3, "scalar")
+        copy_y(8, 0, 1, "scalar")
+        copy_y(9, 0, 1, "scalar")
+        quant_y(8, 0)
+        store_y(9, 2, 3)
+        quant_y(9, 0)
+        copy_y(9, 1, 2, "scalar")
+        turn_y(8, 2, 3)
+        turn_y(8, 1, 2)
+        store_y(8, 1, 2)
+        store_y(8, 2, 3)
         quant_y(9, 1)
+        store_scales(0, 8)
+        turn_y(9, 2, 3)
+        copy_y(9, 2, 3, "vector")
+        copy_y(8, 2, 3, "scalar")
+        copy_y(8, 1, 2, "scalar")
+        quant_y(8, 1)
+        quant_y(9, 2)
+        quant_y(8, 2)
+        store_codes(4, 8)
         store_codes(8, 10)
         store_scales(8, 10)

@@ -66,7 +66,7 @@ def tile_harmonic_phenology_anomaly_k6_kernel(
         wh_scales = keep.tile([P, Q], U8, name="wh_scales", align_bytes=64)
         y_codes = keep.tile([P, GQ, NPIX], U32, name="y_codes", align_bytes=64)
         y_scales = keep.tile([P, GQ, NPIX], U8, name="y_scales", align_bytes=64)
-        w_grouped = keep.tile([P, GT + GQ, 4 * KP], BF16, name="w_grouped", align_bytes=64)
+        w_grouped = keep.tile([P, GT, 4 * KP], BF16, name="w_grouped", align_bytes=64)
 
 
         def px(i):
@@ -76,15 +76,15 @@ def tile_harmonic_phenology_anomaly_k6_kernel(
             return slice(g * KP, (g + 1) * KP)
 
         def load_series(i):
-            t["series", i] = work.tile([P, T], BF16, name="series_t", bufs=4)
+            t["series", i] = work.tile([P, T], BF16, name="series_t", bufs=5)
             nc.sync.dma_start(out=t["series", i][:], in_=series[px(i), :])
 
         def load_site(i):
-            t["site", i] = work.tile([P, D], BF16, name="site_t", bufs=4)
+            t["site", i] = work.tile([P, D], BF16, name="site_t", bufs=5)
             nc.sync.dma_start(out=t["site", i][:], in_=site[px(i), :])
 
         def load_held(i):
-            t["held", i] = work.tile([P, Q], BF16, name="held_t", bufs=4)
+            t["held", i] = work.tile([P, Q], BF16, name="held_t", bufs=5)
             nc.sync.dma_start(out=t["held", i][:], in_=held[px(i), :])
 
         def load_wf(g):
@@ -118,12 +118,12 @@ def tile_harmonic_phenology_anomaly_k6_kernel(
 
         def group_wh(g, half, engine):
             cs = slice(64 * half, 64 * half + 64)
-            dst = w_grouped[:, GT + g, :].rearrange("p (c i t) -> p c t i", i=4, t=4)
+            dst = w_grouped[:, g, :].rearrange("p (c i t) -> p c t i", i=4, t=4)
             src = wh_raw[:, :, grp(g)].rearrange("p t (c i) -> p c t i", i=4)
             copy_on(engine, dst[:, cs], src[:, cs])
 
         def quant_wh(g):
-            nc.vector.quantize_mx(out=wh_codes[:, grp(g)].bitcast(FP8X4), scales=wh_scales[:, grp(g)], in_=w_grouped[:, GT + g, :])
+            nc.vector.quantize_mx(out=wh_codes[:, grp(g)].bitcast(FP8X4), scales=wh_scales[:, grp(g)], in_=w_grouped[:, g, :])
 
         def order_prior():
             for g in range(GD):
@@ -146,7 +146,7 @@ def tile_harmonic_phenology_anomaly_k6_kernel(
                     nc.tensor.transpose(pt[:, col:col + P], words[:, lo + u:lo + 256:2], ident[:])
 
         def copy_x(i, b, engine):
-            if b == 0:
+            if ("xg", i) not in t:
                 t["xg", i] = work.tile([P, T + D], BF16, name="xg", align_bytes=64, bufs=3)
             xg_words = t["xg", i][:].bitcast(F32)
             copy_on(engine,
@@ -202,32 +202,33 @@ def tile_harmonic_phenology_anomaly_k6_kernel(
                                 start=True, stop=True)
 
         def subtract(i, g):
-            if g == 0:
+            if ("diff", i) not in t:
                 t["diff", i] = work.tile([P, Q], F32, name="diff")
             nc.vector.tensor_tensor(out=t["diff", i][:, grp(g)], in0=t["held", i][:, grp(g)], in1=t["curve", i, g][:], op=ALU.subtract)
             give_bank(("curve", i, g))
 
         def bound(i, g0, g1):
-            if g0 == 0:
+            if ("tanh", i) not in t:
                 t["tanh", i] = work.tile([P, Q], F32, name="tanh")
             cols = slice(g0 * KP, g1 * KP)
             nc.scalar.activation(out=t["tanh", i][:, cols], in_=t["diff", i][:, cols], func=ACT.Tanh,
                                  scale=const_cols[:, 4 + i:5 + i])
 
-        def weigh(i, g0, g1):
-            if g0 == 0:
+        def weigh(i, g0, g1, engine):
+            if ("y", i) not in t:
                 t["y", i] = work.tile([P, Q], F32, name="y", bufs=3)
             cols = slice(g0 * KP, g1 * KP)
-            nc.vector.tensor_tensor(out=t["y", i][:, cols], in0=t["tanh", i][:, cols], in1=weight_bc[:, cols], op=ALU.mult)
+            on = nc.vector if engine == "vector" else nc.gpsimd
+            on.tensor_tensor(out=t["y", i][:, cols], in0=t["tanh", i][:, cols], in1=weight_bc[:, cols], op=ALU.mult)
 
         def store_y(i, g0, g1):
             cols = slice(g0 * KP, g1 * KP)
             nc.sync.dma_start(out=out_0[px(i), cols], in_=t["y", i][:, cols])
 
-        def round_y(i, g0, g1, engine):
-            if g0 == 0:
-                t["yb", i] = work.tile([P, Q], BF16, name="yb")
-            pairs = slice(g0 * P, g1 * P)
+        def round_y(i, c0, c1, engine):
+            if ("yb", i) not in t:
+                t["yb", i] = work.tile([P, Q], BF16, name="yb", bufs=3)
+            pairs = slice(c0, c1)
             copy_on(engine,
                     t["yb", i][:].rearrange("m (u c e) -> m u c e", u=2, e=2)[:, :, pairs, :],
                     t["y", i][:].rearrange("m (c u e) -> m u c e", u=2, e=2)[:, :, pairs, :])
@@ -240,7 +241,7 @@ def tile_harmonic_phenology_anomaly_k6_kernel(
                     nc.tensor.transpose(pt[:, px(2 * (g - g0) + u)], words[:, px(GQ * u + g)], ident[:])
 
         def copy_y(i, g0, g1, engine):
-            if g0 == 0:
+            if ("yt", i) not in t:
                 t["yt", i] = work.tile([P, Q], BF16, name="yt", align_bytes=64)
             yt_words = t["yt", i][:].bitcast(F32)
             copy_on(engine,
@@ -269,15 +270,15 @@ def tile_harmonic_phenology_anomaly_k6_kernel(
             copy_on(engine, weight_bc[:, grp(g)], t["wt", g][:, 0:KP])
             give_bank(("wt", g))
 
-        def store_codes(i0, i1):
+        def store_codes(i0, i1, g0, g1):
             cols = slice(i0 * P, i1 * P)
-            dst = out_1.rearrange("g p m t -> p g (m t)")[:, :, 4 * i0 * P:4 * i1 * P].bitcast(I32)
-            nc.sync.dma_start(out=dst, in_=y_codes[:, :, cols].bitcast(I32))
+            dst = out_1.rearrange("g p m t -> p g (m t)")[:, g0:g1, 4 * i0 * P:4 * i1 * P].bitcast(I32)
+            nc.sync.dma_start(out=dst, in_=y_codes[:, g0:g1, cols].bitcast(I32))
 
-        def store_scales(i0, i1):
+        def store_scales(i0, i1, queue):
             cols = slice(i0 * P, i1 * P)
             for q in range(4):
-                nc.sync.dma_start(out=out_2[:, 4 * q:4 * q + 4, cols].rearrange("g r m -> r g m").bitcast(I32),
+                queue.dma_start(out=out_2[:, 4 * q:4 * q + 4, cols].rearrange("g r m -> r g m").bitcast(I32),
                                   in_=y_scales[32 * q:32 * q + 4, :, cols].bitcast(I32))
 
         def load_prior_scales(engine, q):
@@ -299,390 +300,402 @@ def tile_harmonic_phenology_anomaly_k6_kernel(
         for q in range(1, 4):
             load_prior_scales(nc.gpsimd, q)
 
-        turn_consts()
-        copy_consts()
-        load_wf(1)
         load_wf(2)
-        group_wf(0, 0, "scalar")
-        load_series(0)
-        load_series(1)
-        spread_weight(1)
-        load_wf(3)
         load_site(0)
-        group_wf(0, 1, "vector")
-        turn_x(0, 0)
-        group_wf(1, 0, "vector")
-        group_wf(2, 1, "vector")
-        turn_x(0, 1)
-        group_wf(2, 0, "vector")
-        spread_weight(0)
-        load_site(1)
-        quant_wf(0)
-        copy_x(0, 0, "vector")
-        load_series(2)
-        turn_x(1, 0)
-        group_wf(1, 1, "scalar")
-        load_series(3)
-        copy_x(0, 1, "vector")
-        turn_x(1, 1)
-        spread_weight(2)
-        load_prior_words()
-        copy_x(1, 0, "scalar")
-        quant_wf(2)
-        load_wh(1, 3)
-        group_wf(3, 0, "scalar")
-        quant_series(0)
+        group_wf(2, 1, "scalar")
+        turn_consts()
+        load_wf(3)
+        load_series(0)
+        group_wf(0, 0, "scalar")
         turn_x(0, 2)
-        turn_x(1, 2)
-        load_wh(0, 1)
-        load_series(4)
-        copy_weight(1, "scalar")
-        group_wf(3, 1, "vector")
-        copy_x(0, 2, "scalar")
-        copy_x(1, 2, "vector")
+        turn_x(0, 0)
+        load_site(1)
+        turn_x(0, 1)
         load_site(2)
-        copy_x(1, 1, "scalar")
-        quant_wf(3)
-        copy_weight(0, "scalar")
-        quant_wf(1)
-        turn_x(2, 0)
-        turn_x(2, 1)
-        load_held(0)
-        quant_site(0)
-        copy_weight(2, "scalar")
-        order_prior()
-        copy_x(2, 0, "scalar")
-        load_site(3)
-        load_site(4)
-        turn_x(3, 1)
-        quant_series(1)
-        copy_x(2, 1, "scalar")
-        quant_site(1)
-        load_series(5)
-        quant_series(2)
-        turn_x(3, 0)
-        stage1(0)
-        group_wh(1, 1, "vector")
-        stage1(1)
-        group_wh(2, 1, "vector")
-        group_wh(0, 1, "vector")
-        turn_x(4, 1)
-        turn_x(4, 0)
-        group_wh(1, 0, "scalar")
-        group_wh(0, 0, "scalar")
-        copy_x(3, 0, "scalar")
-        shrink_coef(0)
-        quant_wh(1)
-        group_wh(2, 0, "scalar")
-        quant_wh(0)
+        group_wf(3, 0, "vector")
+        copy_consts()
+        group_wf(0, 1, "vector")
+        quant_wf(0)
+        turn_x(1, 2)
+        load_wf(1)
         turn_x(2, 2)
-        shrink_coef(1)
-        quant_coef(0)
+        copy_x(0, 2, "scalar")
+        group_wf(3, 1, "scalar")
+        load_series(1)
+        spread_weight(0)
+        group_wf(2, 0, "vector")
+        spread_weight(2)
+        quant_wf(3)
+        copy_x(0, 0, "vector")
+        turn_x(1, 1)
+        load_series(2)
+        spread_weight(1)
+        copy_x(1, 2, "scalar")
+        group_wf(1, 1, "scalar")
+        load_prior_words()
+        load_wh(1, 3)
+        group_wf(1, 0, "vector")
+        quant_site(0)
+        quant_site(1)
+        quant_wf(2)
+        load_site(3)
+        copy_x(0, 1, "scalar")
+        quant_series(0)
+        load_wh(0, 1)
+        load_series(3)
+        copy_weight(0, "scalar")
+        load_site(4)
+        turn_x(1, 0)
+        quant_wf(1)
+        load_series(4)
+        copy_weight(2, "scalar")
+        copy_x(1, 1, "scalar")
+        order_prior()
+        load_held(0)
+        turn_x(2, 1)
+        copy_x(1, 0, "vector")
+        quant_series(1)
+        turn_x(2, 0)
+        group_wh(2, 1, "vector")
+        group_wh(2, 0, "vector")
+        copy_weight(1, "scalar")
         quant_wh(2)
-        curve(0, 0)
-        copy_x(3, 1, "scalar")
-        curve(0, 1)
-        copy_x(4, 0, "scalar")
         copy_x(2, 2, "scalar")
-        load_held(1)
-        quant_series(3)
-        quant_coef(1)
-        curve(0, 2)
-        turn_x(3, 2)
-        curve(1, 2)
-        curve(1, 0)
-        subtract(0, 0)
-        copy_x(4, 1, "scalar")
-        load_site(5)
-        subtract(0, 2)
-        subtract(0, 1)
-        curve(1, 1)
-        bound(0, 0, 1)
-        subtract(1, 0)
-        turn_x(4, 2)
-        quant_site(2)
-        copy_x(3, 2, "scalar")
-        quant_site(3)
-        bound(0, 1, 2)
-        turn_x(5, 0)
-        subtract(1, 2)
-        bound(0, 2, 3)
-        load_held(2)
-        turn_x(5, 2)
-        subtract(1, 1)
-        stage1(2)
-        bound(1, 0, 1)
-        load_site(6)
-        copy_x(5, 0, "scalar")
-        stage1(3)
-        bound(1, 2, 3)
-        copy_x(4, 2, "scalar")
-        bound(1, 1, 2)
-        weigh(0, 0, 3)
-        shrink_coef(2)
-        round_y(0, 0, 3, "scalar")
-        copy_x(5, 2, "scalar")
+        stage1(0)
+        stage1(1)
+        load_series(5)
+        copy_x(2, 0, "scalar")
+        copy_x(2, 1, "scalar")
         load_series(6)
+        quant_series(2)
+        load_held(1)
+        group_wh(1, 0, "scalar")
+        group_wh(0, 1, "scalar")
+        turn_x(3, 0)
+        shrink_coef(0)
+        quant_coef(0)
+        quant_site(2)
+        turn_x(3, 1)
+        turn_x(3, 2)
+        shrink_coef(1)
+        load_site(5)
+        quant_coef(1)
+        group_wh(1, 1, "scalar")
+        group_wh(0, 0, "scalar")
+        quant_wh(1)
+        turn_x(4, 1)
+        quant_wh(0)
+        curve(0, 2)
+        curve(1, 2)
+        copy_x(3, 0, "scalar")
+        copy_x(3, 2, "scalar")
+        curve(0, 1)
+        curve(0, 0)
+        load_site(6)
+        copy_x(3, 1, "scalar")
+        load_series(7)
+        subtract(0, 2)
+        curve(1, 1)
+        curve(1, 0)
+        bound(0, 2, 3)
+        subtract(0, 1)
+        load_held(2)
+        turn_x(4, 2)
+        quant_site(3)
+        weigh(0, 2, 3, "gpsimd")
+        bound(0, 1, 2)
+        subtract(0, 0)
+        quant_series(3)
+        copy_x(4, 1, "scalar")
+        load_held(3)
+        bound(0, 0, 1)
+        turn_x(4, 0)
+        weigh(0, 0, 2, "gpsimd")
+        load_site(7)
+        subtract(1, 1)
+        subtract(1, 2)
+        stage1(2)
+        copy_x(4, 0, "scalar")
+        stage1(3)
+        shrink_coef(2)
+        subtract(1, 0)
+        bound(1, 1, 2)
+        store_y(0, 0, 3)
+        copy_x(4, 2, "scalar")
+        quant_coef(2)
+        bound(1, 0, 1)
+        bound(1, 2, 3)
         quant_series(4)
         quant_site(4)
-        quant_coef(2)
+        round_y(0, 160, 384, "vector")
+        round_y(0, 0, 160, "scalar")
+        weigh(1, 2, 3, "vector")
+        weigh(1, 0, 2, "gpsimd")
+        round_y(1, 0, 160, "gpsimd")
+        load_series(8)
+        load_site(8)
+        load_held(4)
+        turn_x(5, 0)
         turn_x(5, 1)
-        weigh(1, 0, 3)
+        curve(2, 0)
+        curve(2, 1)
+        curve(2, 2)
+        copy_x(5, 0, "scalar")
+        copy_x(5, 1, "scalar")
+        subtract(2, 0)
+        subtract(2, 1)
+        subtract(2, 2)
+        turn_x(5, 2)
         turn_y(0, 0, 2)
         turn_y(0, 2, 3)
-        copy_x(5, 1, "scalar")
-        curve(2, 0)
-        copy_y(0, 0, 2, "scalar")
-        curve(2, 2)
-        load_held(3)
-        copy_y(0, 2, 3, "scalar")
-        round_y(1, 0, 3, "gpsimd")
-        store_y(0, 0, 3)
-        curve(2, 1)
+        shrink_coef(3)
+        stage1(4)
         store_y(1, 0, 3)
-        load_series(7)
-        load_site(7)
-        load_held(4)
+        bound(2, 0, 1)
+        bound(2, 1, 2)
+        copy_x(5, 2, "scalar")
+        quant_series(5)
+        quant_coef(3)
+        copy_y(0, 0, 2, "scalar")
+        copy_y(0, 2, 3, "scalar")
+        bound(2, 2, 3)
+        round_y(1, 160, 384, "scalar")
+        quant_site(5)
+        weigh(2, 0, 2, "vector")
+        round_y(2, 0, 160, "gpsimd")
+        weigh(2, 2, 3, "gpsimd")
+        load_series(9)
+        load_site(9)
+        load_held(5)
         turn_x(6, 0)
         turn_x(6, 1)
-        subtract(2, 0)
-        bound(2, 0, 1)
-        subtract(2, 1)
-        copy_x(6, 0, "scalar")
-        subtract(2, 2)
-        bound(2, 1, 2)
-        stage1(4)
-        shrink_coef(3)
-        copy_x(6, 1, "scalar")
-        bound(2, 2, 3)
-        quant_y(0, 0)
-        quant_y(0, 1)
-        quant_y(0, 2)
-        quant_coef(3)
-        turn_x(6, 2)
-        turn_y(1, 0, 2)
-        turn_y(1, 2, 3)
-        quant_series(5)
-        quant_site(5)
-        copy_x(6, 2, "scalar")
-        copy_y(1, 0, 2, "scalar")
-        copy_y(1, 2, 3, "scalar")
         curve(3, 0)
         curve(3, 1)
         curve(3, 2)
-        weigh(2, 0, 3)
+        copy_x(6, 0, "scalar")
+        copy_x(6, 1, "scalar")
+        subtract(3, 0)
+        subtract(3, 1)
+        subtract(3, 2)
+        turn_x(6, 2)
+        turn_y(1, 0, 2)
+        turn_y(1, 2, 3)
+        shrink_coef(4)
+        stage1(5)
         store_y(2, 0, 3)
-        round_y(2, 0, 3, "gpsimd")
-        load_series(8)
-        load_site(8)
-        load_held(5)
+        bound(3, 0, 1)
+        bound(3, 1, 2)
+        copy_x(6, 2, "scalar")
+        quant_y(0, 0)
+        quant_series(6)
+        quant_y(0, 1)
+        quant_coef(4)
+        quant_y(0, 2)
+        copy_y(1, 0, 2, "scalar")
+        copy_y(1, 2, 3, "scalar")
+        bound(3, 2, 3)
+        round_y(2, 160, 384, "scalar")
+        quant_site(6)
+        weigh(3, 0, 2, "vector")
+        round_y(3, 0, 160, "gpsimd")
+        weigh(3, 2, 3, "gpsimd")
+        load_held(6)
         turn_x(7, 0)
         turn_x(7, 1)
-        subtract(3, 0)
-        bound(3, 0, 1)
-        subtract(3, 1)
-        copy_x(7, 0, "scalar")
-        subtract(3, 2)
-        bound(3, 1, 2)
-        stage1(5)
-        shrink_coef(4)
-        copy_x(7, 1, "scalar")
-        bound(3, 2, 3)
-        quant_y(1, 0)
-        quant_y(1, 1)
-        quant_y(1, 2)
-        quant_coef(4)
-        turn_x(7, 2)
-        turn_y(2, 0, 2)
-        turn_y(2, 2, 3)
-        quant_series(6)
-        quant_site(6)
-        copy_x(7, 2, "scalar")
-        copy_y(2, 0, 2, "scalar")
-        copy_y(2, 2, 3, "scalar")
         curve(4, 0)
         curve(4, 1)
         curve(4, 2)
-        weigh(3, 0, 3)
+        copy_x(7, 0, "scalar")
+        copy_x(7, 1, "scalar")
+        subtract(4, 0)
+        subtract(4, 1)
+        subtract(4, 2)
+        turn_x(7, 2)
+        turn_y(2, 0, 2)
+        turn_y(2, 2, 3)
+        shrink_coef(5)
+        stage1(6)
         store_y(3, 0, 3)
-        round_y(3, 0, 3, "gpsimd")
-        load_series(9)
-        load_site(9)
-        load_held(6)
+        bound(4, 0, 1)
+        bound(4, 1, 2)
+        copy_x(7, 2, "scalar")
+        quant_y(1, 0)
+        quant_series(7)
+        quant_y(1, 1)
+        quant_coef(5)
+        quant_y(1, 2)
+        copy_y(2, 0, 2, "scalar")
+        copy_y(2, 2, 3, "scalar")
+        bound(4, 2, 3)
+        round_y(3, 160, 384, "scalar")
+        quant_site(7)
+        weigh(4, 0, 2, "vector")
+        round_y(4, 0, 160, "gpsimd")
+        weigh(4, 2, 3, "gpsimd")
+        load_held(7)
         turn_x(8, 0)
         turn_x(8, 1)
-        subtract(4, 0)
-        bound(4, 0, 1)
-        subtract(4, 1)
-        copy_x(8, 0, "scalar")
-        subtract(4, 2)
-        bound(4, 1, 2)
-        stage1(6)
-        shrink_coef(5)
-        copy_x(8, 1, "scalar")
-        bound(4, 2, 3)
-        quant_y(2, 0)
-        quant_y(2, 1)
-        quant_y(2, 2)
-        quant_coef(5)
-        turn_x(8, 2)
-        turn_y(3, 0, 2)
-        turn_y(3, 2, 3)
-        quant_series(7)
-        quant_site(7)
-        copy_x(8, 2, "scalar")
-        copy_y(3, 0, 2, "scalar")
-        copy_y(3, 2, 3, "scalar")
         curve(5, 0)
         curve(5, 1)
         curve(5, 2)
-        weigh(4, 0, 3)
+        copy_x(8, 0, "scalar")
+        copy_x(8, 1, "scalar")
+        subtract(5, 0)
+        subtract(5, 1)
+        subtract(5, 2)
+        turn_x(8, 2)
+        turn_y(3, 0, 2)
+        turn_y(3, 2, 3)
+        shrink_coef(6)
+        stage1(7)
         store_y(4, 0, 3)
-        round_y(4, 0, 3, "gpsimd")
-        load_held(7)
+        bound(5, 0, 1)
+        bound(5, 1, 2)
+        copy_x(8, 2, "scalar")
+        quant_y(2, 0)
+        quant_series(8)
+        quant_y(2, 1)
+        quant_coef(6)
+        quant_y(2, 2)
+        copy_y(3, 0, 2, "scalar")
+        copy_y(3, 2, 3, "scalar")
+        bound(5, 2, 3)
+        round_y(4, 160, 384, "scalar")
+        quant_site(8)
+        weigh(5, 0, 2, "vector")
+        round_y(5, 0, 160, "gpsimd")
+        weigh(5, 2, 3, "gpsimd")
+        load_held(8)
         turn_x(9, 0)
         turn_x(9, 1)
-        subtract(5, 0)
-        bound(5, 0, 1)
-        subtract(5, 1)
-        copy_x(9, 0, "scalar")
-        subtract(5, 2)
-        bound(5, 1, 2)
-        stage1(7)
-        shrink_coef(6)
-        copy_x(9, 1, "scalar")
-        bound(5, 2, 3)
-        quant_y(3, 0)
-        quant_y(3, 1)
-        quant_y(3, 2)
-        store_codes(0, 4)
-        quant_coef(6)
-        turn_x(9, 2)
-        turn_y(4, 0, 2)
-        turn_y(4, 2, 3)
-        quant_series(8)
-        quant_site(8)
-        copy_x(9, 2, "scalar")
-        copy_y(4, 0, 2, "scalar")
-        copy_y(4, 2, 3, "scalar")
         curve(6, 0)
         curve(6, 1)
         curve(6, 2)
-        weigh(5, 0, 3)
-        store_y(5, 0, 3)
-        round_y(5, 0, 3, "gpsimd")
-        load_held(8)
+        copy_x(9, 0, "scalar")
+        copy_x(9, 1, "scalar")
         subtract(6, 0)
-        bound(6, 0, 1)
         subtract(6, 1)
         subtract(6, 2)
-        bound(6, 1, 2)
-        stage1(8)
+        turn_x(9, 2)
+        turn_y(4, 0, 2)
+        turn_y(4, 2, 3)
         shrink_coef(7)
-        bound(6, 2, 3)
-        quant_y(4, 0)
-        quant_y(4, 1)
-        quant_y(4, 2)
-        quant_coef(7)
-        turn_y(5, 0, 2)
-        turn_y(5, 2, 3)
+        stage1(8)
+        store_y(5, 0, 3)
+        bound(6, 0, 1)
+        bound(6, 1, 2)
+        copy_x(9, 2, "scalar")
+        quant_y(3, 0)
         quant_series(9)
+        quant_y(3, 1)
+        quant_coef(7)
+        quant_y(3, 2)
+        store_codes(0, 4, 0, 3)
+        copy_y(4, 0, 2, "scalar")
+        copy_y(4, 2, 3, "scalar")
+        bound(6, 2, 3)
+        round_y(5, 160, 384, "scalar")
         quant_site(9)
-        copy_y(5, 0, 2, "scalar")
-        copy_y(5, 2, 3, "scalar")
+        weigh(6, 0, 2, "vector")
+        round_y(6, 0, 160, "gpsimd")
+        weigh(6, 2, 3, "gpsimd")
+        load_held(9)
         curve(7, 0)
         curve(7, 1)
         curve(7, 2)
-        weigh(6, 0, 3)
-        store_y(6, 0, 3)
-        round_y(6, 0, 3, "gpsimd")
-        shrink_coef(8)
-        load_held(9)
         subtract(7, 0)
-        subtract(7, 2)
         subtract(7, 1)
-        quant_coef(8)
-        bound(7, 0, 1)
+        subtract(7, 2)
+        turn_y(5, 0, 2)
+        turn_y(5, 2, 3)
+        shrink_coef(8)
         stage1(9)
-        shrink_coef(9)
-        bound(7, 2, 3)
-        turn_y(6, 0, 2)
-        turn_y(6, 2, 3)
-        quant_y(5, 1)
-        quant_y(5, 0)
+        store_y(6, 0, 3)
+        bound(7, 0, 1)
         bound(7, 1, 2)
-        copy_y(6, 0, 2, "scalar")
+        quant_y(4, 0)
+        quant_y(4, 1)
+        quant_coef(8)
+        quant_y(4, 2)
+        copy_y(5, 0, 2, "scalar")
+        copy_y(5, 2, 3, "scalar")
+        bound(7, 2, 3)
+        round_y(6, 160, 384, "scalar")
+        weigh(7, 0, 2, "vector")
+        round_y(7, 0, 160, "gpsimd")
+        weigh(7, 2, 3, "gpsimd")
+        quant_y(5, 1)
+        curve(8, 1)
+        curve(8, 2)
+        turn_y(6, 2, 3)
+        quant_y(5, 2)
+        shrink_coef(9)
+        turn_y(6, 0, 2)
         curve(8, 0)
         quant_coef(9)
-        weigh(7, 0, 3)
-        quant_y(5, 2)
-        subtract(8, 0)
-        round_y(7, 0, 3, "gpsimd")
-        curve(8, 2)
-        store_y(7, 0, 3)
-        copy_y(6, 2, 3, "scalar")
-        curve(9, 0)
-        subtract(9, 0)
-        bound(8, 0, 1)
-        curve(8, 1)
-        curve(9, 2)
-        curve(9, 1)
-        bound(9, 0, 1)
-        subtract(9, 1)
-        turn_y(7, 0, 2)
-        turn_y(7, 2, 3)
-        bound(9, 1, 2)
-        subtract(9, 2)
-        weigh(8, 0, 1)
-        round_y(8, 0, 1, "gpsimd")
-        bound(9, 2, 3)
-        weigh(9, 0, 1)
-        turn_y(8, 0, 1)
-        copy_y(7, 0, 2, "scalar")
-        subtract(8, 1)
-        copy_y(7, 2, 3, "scalar")
-        round_y(9, 0, 1, "scalar")
         subtract(8, 2)
-        weigh(9, 1, 2)
-        bound(8, 1, 2)
+        subtract(8, 0)
+        curve(9, 2)
+        copy_y(6, 2, 3, "scalar")
         bound(8, 2, 3)
-        weigh(9, 2, 3)
-        weigh(8, 1, 2)
-        store_y(8, 0, 1)
-        weigh(8, 2, 3)
-        quant_y(6, 2)
-        round_y(9, 2, 3, "gpsimd")
-        quant_y(7, 1)
-        round_y(9, 1, 2, "scalar")
-        store_y(9, 0, 1)
-        round_y(8, 1, 2, "scalar")
-        turn_y(9, 0, 1)
-        store_y(9, 1, 2)
-        quant_y(6, 1)
-        turn_y(9, 1, 2)
-        quant_y(7, 0)
-        quant_y(6, 0)
-        quant_y(7, 2)
-        round_y(8, 2, 3, "scalar")
-        copy_y(8, 0, 1, "scalar")
-        copy_y(9, 0, 1, "scalar")
-        quant_y(8, 0)
+        bound(8, 0, 1)
+        curve(9, 1)
+        subtract(9, 2)
+        subtract(8, 1)
+        bound(9, 2, 3)
+        store_y(7, 0, 3)
+        curve(9, 0)
+        weigh(8, 2, 3, "gpsimd")
+        bound(8, 1, 2)
+        round_y(7, 160, 384, "scalar")
+        subtract(9, 0)
+        turn_y(7, 2, 3)
+        weigh(9, 2, 3, "vector")
+        copy_y(6, 0, 2, "scalar")
+        weigh(8, 0, 2, "vector")
+        bound(9, 0, 1)
+        turn_y(7, 0, 2)
+        subtract(9, 1)
+        bound(9, 1, 2)
         store_y(9, 2, 3)
-        quant_y(9, 0)
-        copy_y(9, 1, 2, "scalar")
+        quant_y(6, 0)
+        quant_y(6, 2)
+        quant_y(5, 0)
+        weigh(9, 0, 1, "vector")
+        round_y(8, 160, 384, "vector")
+        copy_y(7, 0, 2, "scalar")
+        copy_y(7, 2, 3, "scalar")
+        store_y(8, 0, 3)
+        round_y(8, 0, 160, "scalar")
         turn_y(8, 2, 3)
-        turn_y(8, 1, 2)
-        store_y(8, 1, 2)
-        store_y(8, 2, 3)
-        quant_y(9, 1)
-        store_scales(0, 8)
+        weigh(9, 1, 2, "vector")
+        store_y(9, 0, 1)
+        round_y(9, 128, 256, "gpsimd")
+        quant_y(7, 1)
+        quant_y(7, 2)
+        quant_y(6, 1)
+        round_y(9, 0, 128, "scalar")
+        turn_y(8, 0, 2)
+        quant_y(7, 0)
+        copy_y(8, 0, 2, "vector")
+        store_y(9, 1, 2)
+        turn_y(9, 0, 1)
+        turn_y(9, 1, 2)
+        copy_y(9, 0, 1, "vector")
+        copy_y(8, 2, 3, "vector")
+        store_codes(4, 8, 0, 3)
+        round_y(9, 256, 384, "scalar")
         turn_y(9, 2, 3)
-        copy_y(9, 2, 3, "vector")
-        copy_y(8, 2, 3, "scalar")
-        copy_y(8, 1, 2, "scalar")
+        copy_y(9, 1, 2, "scalar")
         quant_y(8, 1)
-        quant_y(9, 2)
+        store_scales(0, 8, nc.sync)
         quant_y(8, 2)
-        store_codes(4, 8)
-        store_codes(8, 10)
-        store_scales(8, 10)
+        quant_y(9, 1)
+        store_codes(8, 10, 1, 2)
+        copy_y(9, 2, 3, "scalar")
+        quant_y(9, 2)
+        store_codes(8, 10, 2, 3)
+        quant_y(8, 0)
+        quant_y(9, 0)
+        store_codes(8, 10, 0, 1)
+        store_scales(8, 10, nc.scalar)

@@ -285,417 +285,421 @@ def tile_harmonic_phenology_anomaly_k6_kernel(
             engine.dma_start(out=ps_raw[32 * q:32 * q + 4, :, :].bitcast(I32),
                              in_=prior_scales[:, 4 * q:4 * q + 4, :].rearrange("g r n -> r g n").bitcast(I32))
 
-        nc.vector.memset(const_rows[:], 0.0)
+        def load_consts():
+            nc.sync.dma_start(out=const_rows[0:4, :].rearrange("t (a r) -> t a r", r=4),
+                              in_=shrink.rearrange("(a t r) -> t a r", t=4, r=4))
+            nc.sync.dma_start(out=const_rows[4:4 + TILES, :], in_=inv_spread.rearrange("(i p) -> i p", p=P))
+            nc.sync.dma_start(out=const_rows[16:16 + Q // P, :], in_=date_weight.rearrange("(i p) -> i p", p=P))
+
         nc.vector.memset(ps_raw[:].bitcast(I32), 0)
+        nc.vector.memset(const_rows[:], 0.0)
         nc.vector.memset(warm[:], 0.0)
         make_identity(nc, ident[:])
         nc.vector.tensor_copy(out=ident_bf[:], in_=ident[:])
         load_wf(0)
-        nc.scalar.dma_start(out=const_rows[0:4, :].rearrange("t (a r) -> t a r", r=4),
-                            in_=shrink.rearrange("(a t r) -> t a r", t=4, r=4))
-        nc.scalar.dma_start(out=const_rows[4:4 + TILES, :], in_=inv_spread.rearrange("(i p) -> i p", p=P))
-        nc.scalar.dma_start(out=const_rows[16:16 + Q // P, :], in_=date_weight.rearrange("(i p) -> i p", p=P))
-        load_prior_scales(nc.scalar, 0)
         nc.scalar.activation(out=warm[:, 4:5], in_=warm[:, 0:1], func=ACT.Tanh)
         for q in range(1, 4):
             load_prior_scales(nc.gpsimd, q)
 
-        load_wf(2)
-        load_site(0)
-        group_wf(2, 1, "scalar")
-        turn_consts()
         load_wf(3)
-        load_series(0)
-        group_wf(0, 0, "scalar")
-        turn_x(0, 2)
-        turn_x(0, 0)
-        load_site(1)
-        turn_x(0, 1)
-        load_site(2)
-        group_wf(3, 0, "vector")
-        copy_consts()
-        group_wf(0, 1, "vector")
-        quant_wf(0)
-        turn_x(1, 2)
+        group_wf(0, 0, "vector")
+        group_wf(3, 1, "vector")
+        load_site(0)
         load_wf(1)
-        turn_x(2, 2)
-        copy_x(0, 2, "scalar")
-        group_wf(3, 1, "scalar")
-        load_series(1)
-        spread_weight(0)
-        group_wf(2, 0, "vector")
-        spread_weight(2)
+        load_series(0)
+        load_consts()
+        turn_x(0, 2)
+        group_wf(3, 0, "scalar")
+        group_wf(0, 1, "vector")
+        load_prior_scales(nc.sync, 0)
         quant_wf(3)
-        copy_x(0, 0, "vector")
-        turn_x(1, 1)
-        load_series(2)
-        spread_weight(1)
-        copy_x(1, 2, "scalar")
+        turn_consts()
+        quant_wf(0)
+        copy_x(0, 2, "scalar")
+        load_wf(2)
+        load_site(1)
+        load_series(1)
         group_wf(1, 1, "scalar")
-        load_prior_words()
-        load_wh(1, 3)
         group_wf(1, 0, "vector")
+        turn_x(0, 0)
+        copy_consts()
+        copy_x(0, 0, "scalar")
         quant_site(0)
-        quant_site(1)
+        group_wf(2, 0, "vector")
+        quant_wf(1)
+        turn_x(0, 1)
+        load_prior_words()
+        group_wf(2, 1, "scalar")
+        turn_x(1, 2)
+        spread_weight(1)
         quant_wf(2)
-        load_site(3)
+        load_wh(0, 1)
+        turn_x(1, 1)
+        load_wh(1, 3)
         copy_x(0, 1, "scalar")
         quant_series(0)
-        load_wh(0, 1)
-        load_series(3)
-        copy_weight(0, "scalar")
-        load_site(4)
         turn_x(1, 0)
-        quant_wf(1)
-        load_series(4)
-        copy_weight(2, "scalar")
-        copy_x(1, 1, "scalar")
         order_prior()
+        group_wh(0, 0, "vector")
+        copy_x(1, 2, "scalar")
+        copy_x(1, 1, "scalar")
+        load_series(2)
+        quant_site(1)
+        copy_x(1, 0, "scalar")
         load_held(0)
-        turn_x(2, 1)
-        copy_x(1, 0, "vector")
-        quant_series(1)
-        turn_x(2, 0)
-        group_wh(2, 1, "vector")
-        group_wh(2, 0, "vector")
-        copy_weight(1, "scalar")
-        quant_wh(2)
-        copy_x(2, 2, "scalar")
-        stage1(0)
-        stage1(1)
-        load_series(5)
-        copy_x(2, 0, "scalar")
-        copy_x(2, 1, "scalar")
-        load_series(6)
-        quant_series(2)
-        load_held(1)
-        group_wh(1, 0, "scalar")
         group_wh(0, 1, "scalar")
-        turn_x(3, 0)
-        shrink_coef(0)
-        quant_coef(0)
-        quant_site(2)
-        turn_x(3, 1)
-        turn_x(3, 2)
-        shrink_coef(1)
-        load_site(5)
-        quant_coef(1)
+        quant_series(1)
+        copy_weight(1, "scalar")
+        stage1(0)
         group_wh(1, 1, "scalar")
-        group_wh(0, 0, "scalar")
-        quant_wh(1)
-        turn_x(4, 1)
+        load_series(3)
+        load_site(2)
+        load_site(3)
         quant_wh(0)
-        curve(0, 2)
-        curve(1, 2)
-        copy_x(3, 0, "scalar")
-        copy_x(3, 2, "scalar")
-        curve(0, 1)
+        group_wh(1, 0, "vector")
+        load_held(1)
+        shrink_coef(0)
+        stage1(1)
+        quant_coef(0)
+        turn_x(2, 1)
+        group_wh(2, 1, "scalar")
+        quant_wh(1)
+        group_wh(2, 0, "scalar")
+        shrink_coef(1)
+        copy_x(2, 1, "scalar")
+        load_site(4)
         curve(0, 0)
-        load_site(6)
-        copy_x(3, 1, "scalar")
-        load_series(7)
-        subtract(0, 2)
-        curve(1, 1)
-        curve(1, 0)
-        bound(0, 2, 3)
-        subtract(0, 1)
-        load_held(2)
-        turn_x(4, 2)
-        quant_site(3)
-        weigh(0, 2, 3, "gpsimd")
-        bound(0, 1, 2)
+        curve(0, 1)
+        quant_coef(1)
+        load_site(5)
+        turn_x(2, 0)
         subtract(0, 0)
-        quant_series(3)
-        copy_x(4, 1, "scalar")
-        load_held(3)
-        bound(0, 0, 1)
-        turn_x(4, 0)
-        weigh(0, 0, 2, "gpsimd")
-        load_site(7)
-        subtract(1, 1)
-        subtract(1, 2)
-        stage1(2)
-        copy_x(4, 0, "scalar")
-        stage1(3)
-        shrink_coef(2)
+        turn_x(2, 2)
+        quant_wh(2)
+        subtract(0, 1)
+        spread_weight(0)
+        copy_x(2, 0, "scalar")
+        load_series(4)
+        curve(0, 2)
+        load_series(5)
+        load_site(6)
+        copy_x(2, 2, "scalar")
+        quant_series(2)
+        bound(0, 0, 2)
+        load_held(2)
+        copy_weight(0, "scalar")
+        curve(1, 0)
+        quant_site(2)
+        subtract(0, 2)
         subtract(1, 0)
-        bound(1, 1, 2)
+        curve(1, 1)
+        bound(0, 2, 3)
+        weigh(0, 0, 2, "vector")
+        spread_weight(2)
+        turn_x(3, 2)
+        copy_weight(2, "scalar")
+        curve(1, 2)
+        subtract(1, 2)
+        weigh(0, 2, 3, "gpsimd")
+        subtract(1, 1)
+        load_held(3)
+        load_series(6)
         store_y(0, 0, 3)
-        copy_x(4, 2, "scalar")
-        quant_coef(2)
-        bound(1, 0, 1)
+        turn_x(3, 1)
+        copy_x(3, 2, "scalar")
+        turn_x(3, 0)
+        copy_x(3, 1, "scalar")
+        copy_x(3, 0, "scalar")
+        quant_series(3)
+        stage1(2)
+        round_y(0, 0, 48, "scalar")
+        bound(1, 0, 2)
         bound(1, 2, 3)
-        quant_series(4)
-        quant_site(4)
-        round_y(0, 160, 384, "vector")
-        round_y(0, 0, 160, "scalar")
-        weigh(1, 2, 3, "vector")
-        weigh(1, 0, 2, "gpsimd")
-        round_y(1, 0, 160, "gpsimd")
-        load_series(8)
-        load_site(8)
+        quant_site(3)
+        load_series(7)
+        load_site(7)
         load_held(4)
-        turn_x(5, 0)
-        turn_x(5, 1)
+        round_y(0, 136, 384, "scalar")
+        shrink_coef(2)
+        turn_x(4, 0)
+        turn_x(4, 1)
+        round_y(0, 48, 136, "vector")
+        quant_coef(2)
+        copy_x(4, 0, "scalar")
+        copy_x(4, 1, "scalar")
         curve(2, 0)
         curve(2, 1)
         curve(2, 2)
-        copy_x(5, 0, "scalar")
-        copy_x(5, 1, "scalar")
+        weigh(1, 0, 2, "vector")
+        round_y(1, 0, 48, "gpsimd")
+        weigh(1, 2, 3, "gpsimd")
+        turn_x(4, 2)
+        turn_y(0, 0, 2)
         subtract(2, 0)
         subtract(2, 1)
         subtract(2, 2)
-        turn_x(5, 2)
-        turn_y(0, 0, 2)
-        turn_y(0, 2, 3)
-        shrink_coef(3)
-        stage1(4)
+        stage1(3)
+        copy_x(4, 2, "scalar")
+        bound(2, 0, 2)
         store_y(1, 0, 3)
-        bound(2, 0, 1)
-        bound(2, 1, 2)
-        copy_x(5, 2, "scalar")
-        quant_series(5)
-        quant_coef(3)
+        quant_series(4)
         copy_y(0, 0, 2, "scalar")
-        copy_y(0, 2, 3, "scalar")
         bound(2, 2, 3)
-        round_y(1, 160, 384, "scalar")
-        quant_site(5)
-        weigh(2, 0, 2, "vector")
-        round_y(2, 0, 160, "gpsimd")
-        weigh(2, 2, 3, "gpsimd")
-        load_series(9)
-        load_site(9)
+        quant_site(4)
+        load_series(8)
+        load_site(8)
         load_held(5)
-        turn_x(6, 0)
-        turn_x(6, 1)
+        round_y(1, 136, 384, "scalar")
+        shrink_coef(3)
+        turn_x(5, 0)
+        turn_x(5, 1)
+        turn_y(0, 2, 3)
+        round_y(1, 48, 136, "vector")
+        quant_coef(3)
+        copy_x(5, 0, "scalar")
+        copy_x(5, 1, "scalar")
         curve(3, 0)
         curve(3, 1)
         curve(3, 2)
-        copy_x(6, 0, "scalar")
-        copy_x(6, 1, "scalar")
+        quant_y(0, 0)
+        weigh(2, 0, 2, "vector")
+        round_y(2, 0, 48, "gpsimd")
+        weigh(2, 2, 3, "gpsimd")
+        copy_y(0, 2, 3, "scalar")
+        turn_x(5, 2)
+        turn_y(1, 0, 2)
         subtract(3, 0)
         subtract(3, 1)
         subtract(3, 2)
-        turn_x(6, 2)
-        turn_y(1, 0, 2)
-        turn_y(1, 2, 3)
-        shrink_coef(4)
-        stage1(5)
+        stage1(4)
+        copy_x(5, 2, "scalar")
+        bound(3, 0, 2)
         store_y(2, 0, 3)
-        bound(3, 0, 1)
-        bound(3, 1, 2)
-        copy_x(6, 2, "scalar")
-        quant_y(0, 0)
-        quant_series(6)
+        quant_series(5)
         quant_y(0, 1)
-        quant_coef(4)
         quant_y(0, 2)
         copy_y(1, 0, 2, "scalar")
-        copy_y(1, 2, 3, "scalar")
         bound(3, 2, 3)
-        round_y(2, 160, 384, "scalar")
-        quant_site(6)
-        weigh(3, 0, 2, "vector")
-        round_y(3, 0, 160, "gpsimd")
-        weigh(3, 2, 3, "gpsimd")
+        quant_site(5)
+        load_series(9)
+        load_site(9)
         load_held(6)
-        turn_x(7, 0)
-        turn_x(7, 1)
+        round_y(2, 136, 384, "scalar")
+        shrink_coef(4)
+        turn_x(6, 0)
+        turn_x(6, 1)
+        turn_y(1, 2, 3)
+        round_y(2, 48, 136, "vector")
+        quant_coef(4)
+        copy_x(6, 0, "scalar")
+        copy_x(6, 1, "scalar")
         curve(4, 0)
         curve(4, 1)
         curve(4, 2)
-        copy_x(7, 0, "scalar")
-        copy_x(7, 1, "scalar")
+        quant_y(1, 0)
+        weigh(3, 0, 2, "vector")
+        round_y(3, 0, 48, "gpsimd")
+        weigh(3, 2, 3, "gpsimd")
+        copy_y(1, 2, 3, "scalar")
+        turn_x(6, 2)
+        turn_y(2, 0, 2)
         subtract(4, 0)
         subtract(4, 1)
         subtract(4, 2)
-        turn_x(7, 2)
-        turn_y(2, 0, 2)
-        turn_y(2, 2, 3)
-        shrink_coef(5)
-        stage1(6)
+        stage1(5)
+        copy_x(6, 2, "scalar")
+        bound(4, 0, 2)
         store_y(3, 0, 3)
-        bound(4, 0, 1)
-        bound(4, 1, 2)
-        copy_x(7, 2, "scalar")
-        quant_y(1, 0)
-        quant_series(7)
+        quant_series(6)
         quant_y(1, 1)
-        quant_coef(5)
         quant_y(1, 2)
+        store_codes(0, 2, 0, 3)
         copy_y(2, 0, 2, "scalar")
-        copy_y(2, 2, 3, "scalar")
         bound(4, 2, 3)
-        round_y(3, 160, 384, "scalar")
-        quant_site(7)
-        weigh(4, 0, 2, "vector")
-        round_y(4, 0, 160, "gpsimd")
-        weigh(4, 2, 3, "gpsimd")
+        quant_site(6)
         load_held(7)
-        turn_x(8, 0)
-        turn_x(8, 1)
+        round_y(3, 136, 384, "scalar")
+        shrink_coef(5)
+        turn_x(7, 0)
+        turn_x(7, 1)
+        turn_y(2, 2, 3)
+        round_y(3, 48, 136, "vector")
+        quant_coef(5)
+        copy_x(7, 0, "scalar")
+        copy_x(7, 1, "scalar")
         curve(5, 0)
         curve(5, 1)
         curve(5, 2)
-        copy_x(8, 0, "scalar")
-        copy_x(8, 1, "scalar")
+        quant_y(2, 0)
+        weigh(4, 0, 2, "vector")
+        round_y(4, 0, 48, "gpsimd")
+        weigh(4, 2, 3, "gpsimd")
+        copy_y(2, 2, 3, "scalar")
+        turn_x(7, 2)
+        turn_y(3, 0, 2)
         subtract(5, 0)
         subtract(5, 1)
         subtract(5, 2)
-        turn_x(8, 2)
-        turn_y(3, 0, 2)
-        turn_y(3, 2, 3)
-        shrink_coef(6)
-        stage1(7)
+        stage1(6)
+        copy_x(7, 2, "scalar")
+        bound(5, 0, 2)
         store_y(4, 0, 3)
-        bound(5, 0, 1)
-        bound(5, 1, 2)
-        copy_x(8, 2, "scalar")
-        quant_y(2, 0)
-        quant_series(8)
+        quant_series(7)
         quant_y(2, 1)
-        quant_coef(6)
         quant_y(2, 2)
         copy_y(3, 0, 2, "scalar")
-        copy_y(3, 2, 3, "scalar")
         bound(5, 2, 3)
-        round_y(4, 160, 384, "scalar")
-        quant_site(8)
-        weigh(5, 0, 2, "vector")
-        round_y(5, 0, 160, "gpsimd")
-        weigh(5, 2, 3, "gpsimd")
+        quant_site(7)
         load_held(8)
-        turn_x(9, 0)
-        turn_x(9, 1)
+        round_y(4, 136, 384, "scalar")
+        shrink_coef(6)
+        turn_x(8, 0)
+        turn_x(8, 1)
+        turn_y(3, 2, 3)
+        round_y(4, 48, 136, "vector")
+        quant_coef(6)
+        copy_x(8, 0, "scalar")
+        copy_x(8, 1, "scalar")
         curve(6, 0)
         curve(6, 1)
         curve(6, 2)
-        copy_x(9, 0, "scalar")
-        copy_x(9, 1, "scalar")
+        quant_y(3, 0)
+        weigh(5, 0, 2, "vector")
+        round_y(5, 0, 48, "gpsimd")
+        weigh(5, 2, 3, "gpsimd")
+        copy_y(3, 2, 3, "scalar")
+        turn_x(8, 2)
+        turn_y(4, 0, 2)
         subtract(6, 0)
         subtract(6, 1)
         subtract(6, 2)
-        turn_x(9, 2)
-        turn_y(4, 0, 2)
-        turn_y(4, 2, 3)
-        shrink_coef(7)
-        stage1(8)
+        stage1(7)
+        copy_x(8, 2, "scalar")
+        bound(6, 0, 2)
         store_y(5, 0, 3)
-        bound(6, 0, 1)
-        bound(6, 1, 2)
-        copy_x(9, 2, "scalar")
-        quant_y(3, 0)
-        quant_series(9)
+        quant_series(8)
         quant_y(3, 1)
-        quant_coef(7)
         quant_y(3, 2)
-        store_codes(0, 4, 0, 3)
+        store_codes(2, 4, 0, 3)
         copy_y(4, 0, 2, "scalar")
-        copy_y(4, 2, 3, "scalar")
         bound(6, 2, 3)
-        round_y(5, 160, 384, "scalar")
-        quant_site(9)
-        weigh(6, 0, 2, "vector")
-        round_y(6, 0, 160, "gpsimd")
-        weigh(6, 2, 3, "gpsimd")
+        quant_site(8)
         load_held(9)
+        round_y(5, 136, 384, "scalar")
+        shrink_coef(7)
+        turn_x(9, 0)
+        turn_x(9, 1)
+        turn_y(4, 2, 3)
+        round_y(5, 48, 136, "vector")
+        quant_coef(7)
+        copy_x(9, 0, "scalar")
+        copy_x(9, 1, "scalar")
         curve(7, 0)
         curve(7, 1)
         curve(7, 2)
+        quant_y(4, 0)
+        weigh(6, 0, 2, "vector")
+        round_y(6, 0, 48, "gpsimd")
+        weigh(6, 2, 3, "gpsimd")
+        copy_y(4, 2, 3, "scalar")
+        turn_x(9, 2)
+        turn_y(5, 0, 2)
         subtract(7, 0)
         subtract(7, 1)
         subtract(7, 2)
-        turn_y(5, 0, 2)
-        turn_y(5, 2, 3)
-        shrink_coef(8)
-        stage1(9)
+        stage1(8)
+        copy_x(9, 2, "scalar")
+        bound(7, 0, 2)
         store_y(6, 0, 3)
-        bound(7, 0, 1)
-        bound(7, 1, 2)
-        quant_y(4, 0)
+        quant_series(9)
         quant_y(4, 1)
-        quant_coef(8)
         quant_y(4, 2)
         copy_y(5, 0, 2, "scalar")
-        copy_y(5, 2, 3, "scalar")
         bound(7, 2, 3)
-        round_y(6, 160, 384, "scalar")
-        weigh(7, 0, 2, "vector")
-        round_y(7, 0, 160, "gpsimd")
-        weigh(7, 2, 3, "gpsimd")
+        quant_site(9)
+        round_y(6, 48, 136, "gpsimd")
+        shrink_coef(8)
         quant_y(5, 1)
-        curve(8, 1)
+        quant_y(5, 0)
+        stage1(9)
+        quant_coef(8)
+        weigh(7, 0, 2, "vector")
+        weigh(7, 2, 3, "gpsimd")
         curve(8, 2)
-        turn_y(6, 2, 3)
-        quant_y(5, 2)
         shrink_coef(9)
-        turn_y(6, 0, 2)
-        curve(8, 0)
-        quant_coef(9)
+        curve(8, 1)
+        round_y(6, 136, 384, "scalar")
+        turn_y(5, 2, 3)
         subtract(8, 2)
+        turn_y(6, 2, 3)
+        quant_coef(9)
+        curve(8, 0)
+        round_y(7, 0, 48, "gpsimd")
+        round_y(7, 48, 136, "scalar")
+        copy_y(5, 2, 3, "scalar")
+        store_y(7, 0, 3)
+        quant_y(5, 2)
         subtract(8, 0)
         curve(9, 2)
-        copy_y(6, 2, 3, "scalar")
-        bound(8, 2, 3)
-        bound(8, 0, 1)
-        curve(9, 1)
-        subtract(9, 2)
-        subtract(8, 1)
-        bound(9, 2, 3)
-        store_y(7, 0, 3)
+        store_scales(0, 6, nc.sync)
         curve(9, 0)
-        weigh(8, 2, 3, "gpsimd")
-        bound(8, 1, 2)
-        round_y(7, 160, 384, "scalar")
+        subtract(9, 2)
+        bound(8, 2, 3)
+        round_y(7, 136, 384, "scalar")
+        subtract(8, 1)
+        curve(9, 1)
+        turn_y(6, 0, 2)
         subtract(9, 0)
+        weigh(8, 2, 3, "gpsimd")
         turn_y(7, 2, 3)
-        weigh(9, 2, 3, "vector")
-        copy_y(6, 0, 2, "scalar")
-        weigh(8, 0, 2, "vector")
-        bound(9, 0, 1)
-        turn_y(7, 0, 2)
+        store_codes(4, 6, 0, 3)
+        bound(9, 2, 3)
+        weigh(9, 2, 3, "gpsimd")
         subtract(9, 1)
+        copy_y(6, 0, 2, "vector")
+        turn_y(7, 0, 2)
+        bound(8, 0, 2)
+        copy_y(6, 2, 3, "scalar")
         bound(9, 1, 2)
-        store_y(9, 2, 3)
+        bound(9, 0, 1)
+        weigh(8, 0, 2, "vector")
+        round_y(8, 0, 48, "scalar")
         quant_y(6, 0)
-        quant_y(6, 2)
-        quant_y(5, 0)
-        weigh(9, 0, 1, "vector")
-        round_y(8, 160, 384, "vector")
-        copy_y(7, 0, 2, "scalar")
-        copy_y(7, 2, 3, "scalar")
-        store_y(8, 0, 3)
-        round_y(8, 0, 160, "scalar")
-        turn_y(8, 2, 3)
+        store_y(9, 2, 3)
         weigh(9, 1, 2, "vector")
-        store_y(9, 0, 1)
-        round_y(9, 128, 256, "gpsimd")
-        quant_y(7, 1)
-        quant_y(7, 2)
+        round_y(8, 136, 384, "scalar")
+        quant_y(6, 2)
         quant_y(6, 1)
-        round_y(9, 0, 128, "scalar")
-        turn_y(8, 0, 2)
+        copy_y(7, 0, 2, "vector")
+        store_y(8, 0, 3)
+        round_y(8, 48, 136, "scalar")
+        turn_y(8, 2, 3)
+        round_y(9, 128, 256, "gpsimd")
+        weigh(9, 0, 1, "vector")
         quant_y(7, 0)
-        copy_y(8, 0, 2, "vector")
+        copy_y(7, 2, 3, "scalar")
         store_y(9, 1, 2)
-        turn_y(9, 0, 1)
-        turn_y(9, 1, 2)
-        copy_y(9, 0, 1, "vector")
-        copy_y(8, 2, 3, "vector")
-        store_codes(4, 8, 0, 3)
+        quant_y(7, 1)
         round_y(9, 256, 384, "scalar")
-        turn_y(9, 2, 3)
-        copy_y(9, 1, 2, "scalar")
-        quant_y(8, 1)
-        store_scales(0, 8, nc.sync)
+        quant_y(7, 2)
+        store_y(9, 0, 1)
+        turn_y(8, 0, 2)
+        turn_y(9, 1, 2)
+        round_y(9, 0, 128, "vector")
+        copy_y(8, 2, 3, "scalar")
         quant_y(8, 2)
-        quant_y(9, 1)
-        store_codes(8, 10, 1, 2)
-        copy_y(9, 2, 3, "scalar")
-        quant_y(9, 2)
-        store_codes(8, 10, 2, 3)
+        turn_y(9, 2, 3)
+        copy_y(8, 0, 2, "scalar")
+        copy_y(9, 2, 3, "vector")
         quant_y(8, 0)
+        turn_y(9, 0, 1)
+        quant_y(8, 1)
+        store_codes(6, 8, 0, 3)
+        copy_y(9, 1, 2, "scalar")
+        quant_y(9, 2)
+        copy_y(9, 0, 1, "scalar")
+        quant_y(9, 1)
         quant_y(9, 0)
-        store_codes(8, 10, 0, 1)
-        store_scales(8, 10, nc.scalar)
+        store_codes(8, 9, 0, 3)
+        store_scales(6, 10, nc.scalar)
+        store_codes(9, 10, 0, 3)

from contextlib import ExitStack

import concourse.mybir as mybir
from concourse.masks import make_identity

NPIX, T, D, H, Q = 1280, 2048, 1024, 512, 1536
FLOPS = 2 * NPIX * (T * H + D * H + H * Q)

F32 = mybir.dt.float32
BF16 = mybir.dt.bfloat16
I32 = mybir.dt.int32
U32 = mybir.dt.uint32
U8 = mybir.dt.uint8
FP8X4 = mybir.dt.float8_e4m3fn_x4
FP4X4 = mybir.dt.float4_e2m1fn_x4
ALU = mybir.AluOpType
ACT = mybir.ActivationFunctionType

P = 128
KP = 512
TILES = NPIX // P
GT, GD, GQ = T // KP, D // KP, Q // KP


def tile_harmonic_phenology_anomaly_k6_kernel(
    tc, series, waves_fit, site, prior_words, prior_scales, shrink, waves_held, held,
    inv_spread, date_weight, out_0, out_1, out_2,
):
    nc = tc.nc
    with ExitStack() as ctx:
        keep = ctx.enter_context(tc.tile_pool(name="keep", bufs=1))
        work = ctx.enter_context(tc.tile_pool(name="work", bufs=2))
        psum = ctx.enter_context(tc.psum_pool(name="psum", bufs=1))
        ctx.enter_context(tc.manual_schedule())

        t = {}
        free_banks = list(range(8))
        bank_of = {}

        def take_bank(key, dtype=F32):
            k = free_banks.pop(0)
            bank_of[key] = k
            width = 512 if dtype == F32 else 1024
            t[key] = psum.tile([P, width], dtype, name="bank%d" % k, tag="bank%d" % k)
            return t[key]

        def give_bank(key):
            free_banks.append(bank_of[key])

        ident = keep.tile([P, P], F32, name="ident")
        ident_bf = keep.tile([P, P], BF16, name="ident_bf")
        const_rows = keep.tile([P, P], BF16, name="const_rows")
        const_cols = keep.tile([P, 16], F32, name="const_cols")
        weight_cols = keep.tile([P, 16], BF16, name="weight_cols")
        warm = keep.tile([P, 8], F32, name="warm")
        weight_bc = keep.tile([P, Q], BF16, name="weight_bc")
        pw_raw = keep.tile([P, GD, 2 * H], U8, name="pw_raw", align_bytes=64)
        ps_raw = keep.tile([P, GD, H], U8, name="ps_raw", align_bytes=64)
        pw = keep.tile([P, GD, 2 * H], U8, name="pw", align_bytes=64)
        ps = keep.tile([P, GD, H], U8, name="ps", align_bytes=64)
        wf_raw = keep.tile([P, GT, 4, H], BF16, name="wf_raw", align_bytes=64)
        wf_codes = keep.tile([P, GT, H], U32, name="wf_codes", align_bytes=64)
        wf_scales = keep.tile([P, GT, H], U8, name="wf_scales", align_bytes=64)
        wh_raw = keep.tile([P, 4, Q], BF16, name="wh_raw", align_bytes=64)
        wh_codes = keep.tile([P, Q], U32, name="wh_codes", align_bytes=64)
        wh_scales = keep.tile([P, Q], U8, name="wh_scales", align_bytes=64)
        y_codes = keep.tile([P, GQ, NPIX], U32, name="y_codes", align_bytes=64)
        y_scales = keep.tile([P, GQ, NPIX], U8, name="y_scales", align_bytes=64)
        w_grouped = keep.tile([P, GT, 4 * KP], BF16, name="w_grouped", align_bytes=64)


        def px(i):
            return slice(i * P, (i + 1) * P)

        def grp(g):
            return slice(g * KP, (g + 1) * KP)

        def load_series(i):
            t["series", i] = work.tile([P, T], BF16, name="series_t", bufs=5)
            nc.sync.dma_start(out=t["series", i][:], in_=series[px(i), :])

        def load_site(i):
            t["site", i] = work.tile([P, D], BF16, name="site_t", bufs=5)
            nc.sync.dma_start(out=t["site", i][:], in_=site[px(i), :])

        def load_held(i):
            t["held", i] = work.tile([P, Q], BF16, name="held_t", bufs=5)
            nc.sync.dma_start(out=t["held", i][:], in_=held[px(i), :])

        def load_wf(g):
            nc.sync.dma_start(out=wf_raw[:, g, :, :], in_=waves_fit[grp(g), :].rearrange("(p j) h -> p j h", j=4))

        def load_prior_words():
            nc.sync.dma_start(out=pw_raw[:].bitcast(I32), in_=prior_words.rearrange("g p b -> p g b").bitcast(I32))

        def load_wh(g0, g1):
            cols = slice(g0 * KP, g1 * KP)
            rows = waves_held.rearrange("(a t r) q -> r a t q", t=4, r=4)
            for r in range(4):
                nc.sync.dma_start(out=wh_raw[r:P:4, :, cols], in_=rows[r, :, :, cols])

        def copy_on(engine, out, in_):
            if engine == "vector":
                nc.vector.tensor_copy(out=out, in_=in_)
            elif engine == "gpsimd":
                nc.gpsimd.tensor_scalar(out=out, in0=in_, scalar1=1.0, scalar2=-0.0, op0=ALU.mult, op1=ALU.add)
            else:
                nc.scalar.copy(out=out, in_=in_)

        def group_wf(g, half, engine):
            ts = slice(2 * half, 2 * half + 2)
            dst = w_grouped[:, g, :].rearrange("p (t a r j) -> p t a j r", t=4, r=4, j=4)
            src = wf_raw[:, g, :, :].rearrange("p j (a t r) -> p t a j r", t=4, r=4)
            copy_on(engine, dst[:, ts], src[:, ts])

        def quant_wf(g):
            nc.vector.quantize_mx(out=wf_codes[:, g, :].bitcast(FP8X4), scales=wf_scales[:, g, :], in_=w_grouped[:, g, :])

        def group_wh(g, half, engine):
            cs = slice(64 * half, 64 * half + 64)
            dst = w_grouped[:, g, :].rearrange("p (c i t) -> p c t i", i=4, t=4)
            src = wh_raw[:, :, grp(g)].rearrange("p t (c i) -> p c t i", i=4)
            copy_on(engine, dst[:, cs], src[:, cs])

        def quant_wh(g):
            nc.vector.quantize_mx(out=wh_codes[:, grp(g)].bitcast(FP8X4), scales=wh_scales[:, grp(g)], in_=w_grouped[:, g, :])

        def order_prior():
            for g in range(GD):
                nc.vector.tensor_copy(
                    out=pw[:, g, :].bitcast(I32).rearrange("p (t a w) -> p t a w", t=4, w=2),
                    in_=pw_raw[:, g, :].bitcast(I32).rearrange("p (a t w) -> p t a w", t=4, w=2))
            nc.vector.tensor_copy(
                out=ps[:].bitcast(I32).rearrange("p g (t a) -> p g t a", t=4),
                in_=ps_raw[:].bitcast(I32).rearrange("p g (a t) -> p g t a", t=4))

        def turn_x(i, b):
            src = t["series", i] if b < 2 else t["site", i]
            words = src[:].bitcast(F32)
            g0 = 2 * b if b < 2 else 0
            pt = take_bank(("xt", i, b))
            for gg in range(2):
                for u in range(2):
                    lo = 256 * (g0 + gg)
                    col = (2 * gg + u) * P
                    nc.tensor.transpose(pt[:, col:col + P], words[:, lo + u:lo + 256:2], ident[:])

        def copy_x(i, b, engine):
            if ("xg", i) not in t:
                t["xg", i] = work.tile([P, T + D], BF16, name="xg", align_bytes=64, bufs=3)
            xg_words = t["xg", i][:].bitcast(F32)
            copy_on(engine,
                    xg_words[:, 512 * b:512 * (b + 1)].rearrange("p (g m u) -> p g m u", g=2, u=2),
                    t["xt", i, b][:].rearrange("p (g u m) -> p g m u", g=2, u=2))
            give_bank(("xt", i, b))

        def x_tiles(i):
            if ("xc", i) not in t:
                t["xc", i] = work.tile([P, (GT + GD) * P], U32, name="xc", align_bytes=64, bufs=3)
                t["xs", i] = work.tile([P, (GT + GD) * P], U8, name="xs", align_bytes=64, bufs=3)

        def quant_series(i):
            x_tiles(i)
            nc.vector.quantize_mx(out=t["xc", i][:, 0:GT * P].bitcast(FP8X4), scales=t["xs", i][:, 0:GT * P], in_=t["xg", i][:, 0:T])

        def quant_site(i):
            x_tiles(i)
            nc.vector.quantize_mx(out=t["xc", i][:, GT * P:].bitcast(FP8X4), scales=t["xs", i][:, GT * P:], in_=t["xg", i][:, T:])

        def stage1(i):
            acc = take_bank(("acc", i))
            xc, xs = t["xc", i], t["xs", i]
            for s in range(4):
                for g in range(GT + GD):
                    if g < GT:
                        lhsT, lhsT_scale = wf_codes[:, g, px(s)].bitcast(FP8X4), wf_scales[:, g, px(s)]
                    else:
                        lhsT = pw[:, g - GT, 2 * P * s:2 * P * (s + 1)].bitcast(FP4X4)
                        lhsT_scale = ps[:, g - GT, px(s)]
                    nc.tensor.matmul_mx(out=acc[:, px(s)], lhsT=lhsT, lhsT_scale=lhsT_scale,
                                        rhs=xc[:, px(g)].bitcast(FP8X4), rhs_scale=xs[:, px(g)],
                                        start=(g == 0), stop=(g == GT + GD - 1))

        def shrink_coef(i):
            t["coef", i] = work.tile([P, H], BF16, name="coef", align_bytes=64)
            nc.vector.tensor_tensor(
                out=t["coef", i][:].rearrange("p (m s) -> p m s", s=4),
                in0=t["acc", i][:].rearrange("p (s m) -> p m s", s=4),
                in1=const_cols[:, 0:4].unsqueeze(1).to_broadcast([P, P, 4]),
                op=ALU.mult)
            give_bank(("acc", i))

        def quant_coef(i):
            t["cc", i] = work.tile([P, P], U32, name="cc", align_bytes=64, bufs=3)
            t["cs", i] = work.tile([P, P], U8, name="cs", align_bytes=64, bufs=3)
            nc.vector.quantize_mx(out=t["cc", i][:].bitcast(FP8X4), scales=t["cs", i][:], in_=t["coef", i][:])

        def curve(i, g):
            take_bank(("curve", i, g))
            nc.tensor.matmul_mx(out=t["curve", i, g][:], lhsT=t["cc", i][:].bitcast(FP8X4), lhsT_scale=t["cs", i][:],
                                rhs=wh_codes[:, grp(g)].bitcast(FP8X4), rhs_scale=wh_scales[:, grp(g)],
                                start=True, stop=True)

        def subtract(i, g):
            if ("diff", i) not in t:
                t["diff", i] = work.tile([P, Q], F32, name="diff")
            nc.vector.tensor_tensor(out=t["diff", i][:, grp(g)], in0=t["held", i][:, grp(g)], in1=t["curve", i, g][:], op=ALU.subtract)
            give_bank(("curve", i, g))

        def bound(i, g0, g1):
            if ("tanh", i) not in t:
                t["tanh", i] = work.tile([P, Q], F32, name="tanh")
            cols = slice(g0 * KP, g1 * KP)
            nc.scalar.activation(out=t["tanh", i][:, cols], in_=t["diff", i][:, cols], func=ACT.Tanh,
                                 scale=const_cols[:, 4 + i:5 + i])

        def weigh(i, g0, g1, engine):
            if ("y", i) not in t:
                t["y", i] = work.tile([P, Q], F32, name="y", bufs=3)
            cols = slice(g0 * KP, g1 * KP)
            on = nc.vector if engine == "vector" else nc.gpsimd
            on.tensor_tensor(out=t["y", i][:, cols], in0=t["tanh", i][:, cols], in1=weight_bc[:, cols], op=ALU.mult)

        def store_y(i, g0, g1):
            cols = slice(g0 * KP, g1 * KP)
            nc.sync.dma_start(out=out_0[px(i), cols], in_=t["y", i][:, cols])

        def round_y(i, c0, c1, engine):
            if ("yb", i) not in t:
                t["yb", i] = work.tile([P, Q], BF16, name="yb", bufs=3)
            pairs = slice(c0, c1)
            copy_on(engine,
                    t["yb", i][:].rearrange("m (u c e) -> m u c e", u=2, e=2)[:, :, pairs, :],
                    t["y", i][:].rearrange("m (c u e) -> m u c e", u=2, e=2)[:, :, pairs, :])

        def turn_y(i, g0, g1):
            words = t["yb", i][:].bitcast(F32)
            pt = take_bank(("ytp", i, g0))
            for g in range(g0, g1):
                for u in range(2):
                    nc.tensor.transpose(pt[:, px(2 * (g - g0) + u)], words[:, px(GQ * u + g)], ident[:])

        def copy_y(i, g0, g1, engine):
            if ("yt", i) not in t:
                t["yt", i] = work.tile([P, Q], BF16, name="yt", align_bytes=64)
            yt_words = t["yt", i][:].bitcast(F32)
            copy_on(engine,
                    yt_words[:, 2 * g0 * P:2 * g1 * P].rearrange("p (g m u) -> p g m u", m=P, u=2),
                    t["ytp", i, g0][:, 0:2 * (g1 - g0) * P].rearrange("p (g u m) -> p g m u", m=P, u=2))
            give_bank(("ytp", i, g0))

        def quant_y(i, g):
            nc.vector.quantize_mx(out=y_codes[:, g, px(i)].bitcast(FP8X4), scales=y_scales[:, g, px(i)], in_=t["yt", i][:, grp(g)])

        def turn_consts():
            take_bank("consts", BF16)
            nc.tensor.transpose(t["consts"][:, 0:P], const_rows[:], ident_bf[:])

        def copy_consts():
            nc.scalar.copy(out=weight_cols[:], in_=t["consts"][:, 16:32])
            nc.scalar.copy(out=const_cols[:], in_=t["consts"][:, 0:16])
            give_bank("consts")

        def spread_weight(g):
            take_bank(("wt", g), BF16)
            for c in range(4):
                nc.tensor.transpose(t["wt", g][:, px(c)], weight_cols[:, 4 * g + c:4 * g + c + 1].to_broadcast([P, P]), ident_bf[:])

        def copy_weight(g, engine):
            copy_on(engine, weight_bc[:, grp(g)], t["wt", g][:, 0:KP])
            give_bank(("wt", g))

        def store_codes(i0, i1, g0, g1):
            cols = slice(i0 * P, i1 * P)
            dst = out_1.rearrange("g p m t -> p g (m t)")[:, g0:g1, 4 * i0 * P:4 * i1 * P].bitcast(I32)
            nc.sync.dma_start(out=dst, in_=y_codes[:, g0:g1, cols].bitcast(I32))

        def store_scales(i0, i1, queue):
            cols = slice(i0 * P, i1 * P)
            for q in range(4):
                queue.dma_start(out=out_2[:, 4 * q:4 * q + 4, cols].rearrange("g r m -> r g m").bitcast(I32),
                                  in_=y_scales[32 * q:32 * q + 4, :, cols].bitcast(I32))

        def load_prior_scales(engine, q):
            engine.dma_start(out=ps_raw[32 * q:32 * q + 4, :, :].bitcast(I32),
                             in_=prior_scales[:, 4 * q:4 * q + 4, :].rearrange("g r n -> r g n").bitcast(I32))

        def load_consts():
            nc.sync.dma_start(out=const_rows[0:4, :].rearrange("t (a r) -> t a r", r=4),
                              in_=shrink.rearrange("(a t r) -> t a r", t=4, r=4))
            nc.sync.dma_start(out=const_rows[4:4 + TILES, :], in_=inv_spread.rearrange("(i p) -> i p", p=P))
            nc.sync.dma_start(out=const_rows[16:16 + Q // P, :], in_=date_weight.rearrange("(i p) -> i p", p=P))

        nc.vector.memset(ps_raw[:].bitcast(I32), 0)
        nc.vector.memset(const_rows[:], 0.0)
        nc.vector.memset(warm[:], 0.0)
        make_identity(nc, ident[:])
        nc.vector.tensor_copy(out=ident_bf[:], in_=ident[:])
        load_wf(0)
        nc.scalar.activation(out=warm[:, 4:5], in_=warm[:, 0:1], func=ACT.Tanh)
        for q in range(1, 4):
            load_prior_scales(nc.gpsimd, q)

        load_wf(3)
        group_wf(0, 0, "vector")
        group_wf(3, 1, "vector")
        load_site(0)
        load_wf(1)
        load_series(0)
        load_consts()
        turn_x(0, 2)
        group_wf(3, 0, "scalar")
        group_wf(0, 1, "vector")
        load_prior_scales(nc.sync, 0)
        quant_wf(3)
        turn_consts()
        quant_wf(0)
        copy_x(0, 2, "scalar")
        load_wf(2)
        load_site(1)
        load_series(1)
        group_wf(1, 1, "scalar")
        group_wf(1, 0, "vector")
        turn_x(0, 0)
        copy_consts()
        copy_x(0, 0, "scalar")
        quant_site(0)
        group_wf(2, 0, "vector")
        quant_wf(1)
        turn_x(0, 1)
        load_prior_words()
        group_wf(2, 1, "scalar")
        turn_x(1, 2)
        spread_weight(1)
        quant_wf(2)
        load_wh(0, 1)
        turn_x(1, 1)
        load_wh(1, 3)
        copy_x(0, 1, "scalar")
        quant_series(0)
        turn_x(1, 0)
        order_prior()
        group_wh(0, 0, "vector")
        copy_x(1, 2, "scalar")
        copy_x(1, 1, "scalar")
        load_series(2)
        quant_site(1)
        copy_x(1, 0, "scalar")
        load_held(0)
        group_wh(0, 1, "scalar")
        quant_series(1)
        copy_weight(1, "scalar")
        stage1(0)
        group_wh(1, 1, "scalar")
        load_series(3)
        load_site(2)
        load_site(3)
        quant_wh(0)
        group_wh(1, 0, "vector")
        load_held(1)
        shrink_coef(0)
        stage1(1)
        quant_coef(0)
        turn_x(2, 1)
        group_wh(2, 1, "scalar")
        quant_wh(1)
        group_wh(2, 0, "scalar")
        shrink_coef(1)
        copy_x(2, 1, "scalar")
        load_site(4)
        curve(0, 0)
        curve(0, 1)
        quant_coef(1)
        load_site(5)
        turn_x(2, 0)
        subtract(0, 0)
        turn_x(2, 2)
        quant_wh(2)
        subtract(0, 1)
        spread_weight(0)
        copy_x(2, 0, "scalar")
        load_series(4)
        curve(0, 2)
        load_series(5)
        load_site(6)
        copy_x(2, 2, "scalar")
        quant_series(2)
        bound(0, 0, 2)
        load_held(2)
        copy_weight(0, "scalar")
        curve(1, 0)
        quant_site(2)
        subtract(0, 2)
        subtract(1, 0)
        curve(1, 1)
        bound(0, 2, 3)
        weigh(0, 0, 2, "vector")
        spread_weight(2)
        turn_x(3, 2)
        copy_weight(2, "scalar")
        curve(1, 2)
        subtract(1, 2)
        weigh(0, 2, 3, "gpsimd")
        subtract(1, 1)
        load_held(3)
        load_series(6)
        store_y(0, 0, 3)
        turn_x(3, 1)
        copy_x(3, 2, "scalar")
        turn_x(3, 0)
        copy_x(3, 1, "scalar")
        copy_x(3, 0, "scalar")
        quant_series(3)
        stage1(2)
        round_y(0, 0, 48, "scalar")
        bound(1, 0, 2)
        bound(1, 2, 3)
        quant_site(3)
        load_series(7)
        load_site(7)
        load_held(4)
        round_y(0, 136, 384, "scalar")
        shrink_coef(2)
        turn_x(4, 0)
        turn_x(4, 1)
        round_y(0, 48, 136, "vector")
        quant_coef(2)
        copy_x(4, 0, "scalar")
        copy_x(4, 1, "scalar")
        curve(2, 0)
        curve(2, 1)
        curve(2, 2)
        weigh(1, 0, 2, "vector")
        round_y(1, 0, 48, "gpsimd")
        weigh(1, 2, 3, "gpsimd")
        turn_x(4, 2)
        turn_y(0, 0, 2)
        subtract(2, 0)
        subtract(2, 1)
        subtract(2, 2)
        stage1(3)
        copy_x(4, 2, "scalar")
        bound(2, 0, 2)
        store_y(1, 0, 3)
        quant_series(4)
        copy_y(0, 0, 2, "scalar")
        bound(2, 2, 3)
        quant_site(4)
        load_series(8)
        load_site(8)
        load_held(5)
        round_y(1, 136, 384, "scalar")
        shrink_coef(3)
        turn_x(5, 0)
        turn_x(5, 1)
        turn_y(0, 2, 3)
        round_y(1, 48, 136, "vector")
        quant_coef(3)
        copy_x(5, 0, "scalar")
        copy_x(5, 1, "scalar")
        curve(3, 0)
        curve(3, 1)
        curve(3, 2)
        quant_y(0, 0)
        weigh(2, 0, 2, "vector")
        round_y(2, 0, 48, "gpsimd")
        weigh(2, 2, 3, "gpsimd")
        copy_y(0, 2, 3, "scalar")
        turn_x(5, 2)
        turn_y(1, 0, 2)
        subtract(3, 0)
        subtract(3, 1)
        subtract(3, 2)
        stage1(4)
        copy_x(5, 2, "scalar")
        bound(3, 0, 2)
        store_y(2, 0, 3)
        quant_series(5)
        quant_y(0, 1)
        quant_y(0, 2)
        copy_y(1, 0, 2, "scalar")
        bound(3, 2, 3)
        quant_site(5)
        load_series(9)
        load_site(9)
        load_held(6)
        round_y(2, 136, 384, "scalar")
        shrink_coef(4)
        turn_x(6, 0)
        turn_x(6, 1)
        turn_y(1, 2, 3)
        round_y(2, 48, 136, "vector")
        quant_coef(4)
        copy_x(6, 0, "scalar")
        copy_x(6, 1, "scalar")
        curve(4, 0)
        curve(4, 1)
        curve(4, 2)
        quant_y(1, 0)
        weigh(3, 0, 2, "vector")
        round_y(3, 0, 48, "gpsimd")
        weigh(3, 2, 3, "gpsimd")
        copy_y(1, 2, 3, "scalar")
        turn_x(6, 2)
        turn_y(2, 0, 2)
        subtract(4, 0)
        subtract(4, 1)
        subtract(4, 2)
        stage1(5)
        copy_x(6, 2, "scalar")
        bound(4, 0, 2)
        store_y(3, 0, 3)
        quant_series(6)
        quant_y(1, 1)
        quant_y(1, 2)
        store_codes(0, 2, 0, 3)
        copy_y(2, 0, 2, "scalar")
        bound(4, 2, 3)
        quant_site(6)
        load_held(7)
        round_y(3, 136, 384, "scalar")
        shrink_coef(5)
        turn_x(7, 0)
        turn_x(7, 1)
        turn_y(2, 2, 3)
        round_y(3, 48, 136, "vector")
        quant_coef(5)
        copy_x(7, 0, "scalar")
        copy_x(7, 1, "scalar")
        curve(5, 0)
        curve(5, 1)
        curve(5, 2)
        quant_y(2, 0)
        weigh(4, 0, 2, "vector")
        round_y(4, 0, 48, "gpsimd")
        weigh(4, 2, 3, "gpsimd")
        copy_y(2, 2, 3, "scalar")
        turn_x(7, 2)
        turn_y(3, 0, 2)
        subtract(5, 0)
        subtract(5, 1)
        subtract(5, 2)
        stage1(6)
        copy_x(7, 2, "scalar")
        bound(5, 0, 2)
        store_y(4, 0, 3)
        quant_series(7)
        quant_y(2, 1)
        quant_y(2, 2)
        copy_y(3, 0, 2, "scalar")
        bound(5, 2, 3)
        quant_site(7)
        load_held(8)
        round_y(4, 136, 384, "scalar")
        shrink_coef(6)
        turn_x(8, 0)
        turn_x(8, 1)
        turn_y(3, 2, 3)
        round_y(4, 48, 136, "vector")
        quant_coef(6)
        copy_x(8, 0, "scalar")
        copy_x(8, 1, "scalar")
        curve(6, 0)
        curve(6, 1)
        curve(6, 2)
        quant_y(3, 0)
        weigh(5, 0, 2, "vector")
        round_y(5, 0, 48, "gpsimd")
        weigh(5, 2, 3, "gpsimd")
        copy_y(3, 2, 3, "scalar")
        turn_x(8, 2)
        turn_y(4, 0, 2)
        subtract(6, 0)
        subtract(6, 1)
        subtract(6, 2)
        stage1(7)
        copy_x(8, 2, "scalar")
        bound(6, 0, 2)
        store_y(5, 0, 3)
        quant_series(8)
        quant_y(3, 1)
        quant_y(3, 2)
        store_codes(2, 4, 0, 3)
        copy_y(4, 0, 2, "scalar")
        bound(6, 2, 3)
        quant_site(8)
        load_held(9)
        round_y(5, 136, 384, "scalar")
        shrink_coef(7)
        turn_x(9, 0)
        turn_x(9, 1)
        turn_y(4, 2, 3)
        round_y(5, 48, 136, "vector")
        quant_coef(7)
        copy_x(9, 0, "scalar")
        copy_x(9, 1, "scalar")
        curve(7, 0)
        curve(7, 1)
        curve(7, 2)
        quant_y(4, 0)
        weigh(6, 0, 2, "vector")
        round_y(6, 0, 48, "gpsimd")
        weigh(6, 2, 3, "gpsimd")
        copy_y(4, 2, 3, "scalar")
        turn_x(9, 2)
        turn_y(5, 0, 2)
        subtract(7, 0)
        subtract(7, 1)
        subtract(7, 2)
        stage1(8)
        copy_x(9, 2, "scalar")
        bound(7, 0, 2)
        store_y(6, 0, 3)
        quant_series(9)
        quant_y(4, 1)
        quant_y(4, 2)
        copy_y(5, 0, 2, "scalar")
        bound(7, 2, 3)
        quant_site(9)
        round_y(6, 48, 136, "gpsimd")
        shrink_coef(8)
        quant_y(5, 1)
        quant_y(5, 0)
        stage1(9)
        quant_coef(8)
        weigh(7, 0, 2, "vector")
        weigh(7, 2, 3, "gpsimd")
        curve(8, 2)
        shrink_coef(9)
        curve(8, 1)
        round_y(6, 136, 384, "scalar")
        turn_y(5, 2, 3)
        subtract(8, 2)
        turn_y(6, 2, 3)
        quant_coef(9)
        curve(8, 0)
        round_y(7, 0, 48, "gpsimd")
        round_y(7, 48, 136, "scalar")
        copy_y(5, 2, 3, "scalar")
        store_y(7, 0, 3)
        quant_y(5, 2)
        subtract(8, 0)
        curve(9, 2)
        store_scales(0, 6, nc.sync)
        curve(9, 0)
        subtract(9, 2)
        bound(8, 2, 3)
        round_y(7, 136, 384, "scalar")
        subtract(8, 1)
        curve(9, 1)
        turn_y(6, 0, 2)
        subtract(9, 0)
        weigh(8, 2, 3, "gpsimd")
        turn_y(7, 2, 3)
        store_codes(4, 6, 0, 3)
        bound(9, 2, 3)
        weigh(9, 2, 3, "gpsimd")
        subtract(9, 1)
        copy_y(6, 0, 2, "vector")
        turn_y(7, 0, 2)
        bound(8, 0, 2)
        copy_y(6, 2, 3, "scalar")
        bound(9, 1, 2)
        bound(9, 0, 1)
        weigh(8, 0, 2, "vector")
        round_y(8, 0, 48, "scalar")
        quant_y(6, 0)
        store_y(9, 2, 3)
        weigh(9, 1, 2, "vector")
        round_y(8, 136, 384, "scalar")
        quant_y(6, 2)
        quant_y(6, 1)
        copy_y(7, 0, 2, "vector")
        store_y(8, 0, 3)
        round_y(8, 48, 136, "scalar")
        turn_y(8, 2, 3)
        round_y(9, 128, 256, "gpsimd")
        weigh(9, 0, 1, "vector")
        quant_y(7, 0)
        copy_y(7, 2, 3, "scalar")
        store_y(9, 1, 2)
        quant_y(7, 1)
        round_y(9, 256, 384, "scalar")
        quant_y(7, 2)
        store_y(9, 0, 1)
        turn_y(8, 0, 2)
        turn_y(9, 1, 2)
        round_y(9, 0, 128, "vector")
        copy_y(8, 2, 3, "scalar")
        quant_y(8, 2)
        turn_y(9, 2, 3)
        copy_y(8, 0, 2, "scalar")
        copy_y(9, 2, 3, "vector")
        quant_y(8, 0)
        turn_y(9, 0, 1)
        quant_y(8, 1)
        store_codes(6, 8, 0, 3)
        copy_y(9, 1, 2, "scalar")
        quant_y(9, 2)
        copy_y(9, 0, 1, "scalar")
        quant_y(9, 1)
        quant_y(9, 0)
        store_codes(8, 9, 0, 3)
        store_scales(6, 10, nc.scalar)
        store_codes(9, 10, 0, 3)
